import numpy as np, ml_dtypes
CORES = [40,64,80,88,96,104,120,144]
N = 8
import mx_ref
BF = ml_dtypes.bfloat16
def gentries(a):
    return np.ascontiguousarray(a.reshape(8, 16, -1).transpose(0, 2, 1)).reshape(8, -1)
def gtable(e):
    e = np.asarray(e); return np.ascontiguousarray(e.reshape(8, -1, 16).transpose(0, 2, 1)).reshape(128, -1).astype(np.int32)
def gcols(t, e):
    v = np.concatenate([t.reshape(8, 16, -1, 4), np.zeros((8, 16, 1, 4), BF)], axis=2)
    return np.ascontiguousarray(np.stack([v[g][:, e[g]] for g in range(8)])).reshape(128, -1)
def tile(rs):
    return np.stack(rs, axis=2).reshape(128, -1).astype(BF)
def pick(q, e):
    c = np.concatenate([q[0].reshape(128, -1, 4), np.zeros((128, 1, 4), np.uint8)], axis=1); s = np.concatenate([q[1], np.ones((16, 1), np.uint8)], axis=1)
    return (np.ascontiguousarray(c[:, e].reshape(128, -1)), np.ascontiguousarray(s[:, e]))
def join(*qs):
    return (np.concatenate([q[0] for q in qs], axis=1), np.concatenate([q[1] for q in qs], axis=1))
def put(q, e, v):
    c, s = q[0].reshape(128, -1, 4).copy(), q[1].copy(); c[:, e] = v[0].reshape(128, -1, 4); s[:, e] = v[1]
    return (c.reshape(128, -1), s)
def pk(c, s):
    return (np.ascontiguousarray(c), mx_ref.live(s))
def emit(q):
    return q[0], q[1]
def packed(v, rng):
    q = [mx_ref.quantize(np.ascontiguousarray(v[r])) for r in range(N)]
    return np.stack([a for a, b in q]), np.stack([mx_ref.plane(b, rng) for a, b in q])
def values_of_codes():
    e, c = np.zeros((128, 128, 4), np.float32), np.zeros((128, 2, 4), np.uint8)
    e[np.arange(128), np.arange(128), 0] = 1
    c[:127, :, 0] = np.arange(256).reshape(2, 128).T[:127]
    return mx_ref.matmul(mx_ref.quantize(e.reshape(128, 512).astype(BF)), (c.reshape(128, 8), np.full((16, 2), 127, np.uint8))).T.reshape(-1).astype(np.float64)
CODE_VALUE, SCALE_VALUE = values_of_codes(), 2.0 ** (np.arange(256) - 127.0)
def decode(q):
    return (CODE_VALUE[q[0]].reshape(16, 8, -1, 4) * SCALE_VALUE[q[1]][:, None, :, None] + 0.0).reshape(128, -1).astype(np.float32)
def f(rng, *shape):
    return mx_ref.flush((rng.standard_normal(shape, dtype=np.float32) * np.exp2(rng.integers(-2, 3, shape[:-1] + (1,)))).astype(BF))
def wide(rng, *shape, cols=0):
    v = rng.standard_normal(shape, dtype=np.float32) * np.exp2(rng.integers(-12, 13, shape)).astype(np.float32)
    if cols: v *= np.repeat(np.exp2(rng.integers(-cols, cols + 1, shape[:-2] + (1, shape[-1] // 4))) * (rng.random(shape[:-2] + (1, shape[-1] // 4)) > 0.0625), 4, axis=-1).astype(np.float32)
    return mx_ref.flush(v.astype(BF))
C = 352
MASK = [2, 4, 1]
ALIKE = 1
def numbers_of(rng):
    return {"x": np.array(f(rng, N, 128, 4 * C)), "u": np.array(f(rng, N, 128, 512)), "v": np.array(f(rng, N, 128, 512))}
def stored(k):
    return {"se": np.stack([gtable(k[r].reshape(8, 2 * C)) for r in range(N)])}
def lists(rng):
    return stored(rng.permuted(np.tile(np.arange(C), (N, 8, 2, 1)), axis=3))
def layers(rng):
    return np.array(f(rng, N, 128, 2048)).reshape(N, 8, 16, 4, 8, 16, 4)
def weights(rng, w):
    c, s = packed(np.ascontiguousarray(w).reshape(N, 128, 2048), rng)
    return {"wc": c, "ws": s}
def setup_inputs(rng):
    return {**numbers_of(rng), **lists(rng), **weights(rng, layers(rng))}
def setup_inputs_ties(rng):
    d = numbers_of(rng)
    o = rng.permutation(N)
    k = rng.integers(-1, 2, (N, 8, 7, C)).astype(np.float32)
    k[o[1]] = 1
    x = d["x"].reshape(N, 8, 16, C, 4)
    x[:, :, :7, :, 0] = k.astype(BF)
    x[:, :, 8:] = 0
    a = np.exp2(rng.integers(-3, 4, (8, 1)).astype(np.float32))
    x[:, :, 8, :, 0] = (-3.0 * a).astype(BF)
    x[:, :, 10, :, 0] = (-0.0625 * a).astype(BF)
    x[:, :, 11, :, 0] = (0.28125 * a).astype(BF)
    c = np.ones(N, np.float32)
    c[o[0]] = 0
    c[o[2]] = -1
    u = d["u"].reshape(N, 128, 128, 4)
    for l in range(7):
        u[:, :, l::16] = 0
        for h in range(0, 128, 16): u[:, h + l, h + l, 0] = c.astype(BF)
    w = layers(rng)
    w[:, :, :, 0, :, :7] = 0
    w[:, :, :, :, :, 8:] = 0
    for g in range(8):
        w[:, g, 11, 0, g, 8, 0] = 112.0
        for b in range(4): w[:, g, 10, b, g, 9, 0] = -(1.125 + 0.25 * b) * 2.0 ** -5
    return {"x": x.reshape(N, 128, 4 * C), "u": u.reshape(N, 128, 512), "v": d["v"], **lists(rng), **weights(rng, w)}
def setup_inputs_near(rng):
    d = numbers_of(rng)
    k = np.where(((np.arange(N) & ALIKE) > 0) ^ (rng.random() < 0.5), 2.0 ** -30, 1.0)
    x = np.zeros((N, 8, 16, C, 4))
    s = rng.integers(-1, 2, (N, 8, 7, C)) * k[:, None, None, None]
    x[:, :, :7, :, 0] = 1.125 * s
    x[:, :, 8:15, :, 0] = -1.25 * s
    x[:, :, 15] = rng.choice([-1.0, 1.0], (N, 8, C, 4)) * (1.0 + 0.125 * rng.integers(0, 8, (N, 8, C, 4)) * (np.arange(4) > 1)) * 2.0 ** -30
    x[:, :, 15, :, 1] = 2.0 ** -30
    x[:, :, 7, :, 0] = 2.0 ** -30
    for r in range(N):
        at = [0, C - 1, int(rng.integers(C)), int(rng.integers(C))]
        for g, j in zip(rng.permutation(8)[:4], at): x[r, g, int(rng.integers(7)), j, 0] = 2.0 ** 30 * rng.choice([-1.0, 1.0])
    u = d["u"].reshape(N, 128, 128, 4)
    w = np.zeros((N, 8, 16, 4, 8, 16, 4), np.float32)
    for g in range(8):
        w[:, g, 15, 1, g, 7, 0] = 32.0
        w[:, g, 15, 1, g, 15, 1] = 32.0
        w[:, g, 15, 2:, g, 15, 2:] = rng.choice([-1.0, 1.0], (N, 2, 2)) * (8.0 + rng.integers(0, 8, (N, 2, 2)))
    for l in range(7):
        u[:, :, l::16] = 0
        for g in range(8):
            h = 16 * g
            u[:, h + l, h + l, 0] = (1.125 * k).astype(np.float32).astype(BF)
            u[:, h + 8 + l, h + l, 0] = k.astype(np.float32).astype(BF)
            w[:, g, 15, 0, g, l, 0] = rng.choice([-1.0, 1.0], N) * 2.0 ** -8
    return {"x": x.astype(np.float32).reshape(N, 128, 4 * C).astype(BF), "u": u.reshape(N, 128, 512), "v": d["v"], **lists(rng), **weights(rng, w.astype(BF))}
def setup_inputs_odd(rng):
    d = numbers_of(rng)
    x = (1.0 + (2 * rng.integers(0, 64, (N, 8, 16, C, 4)) + 1) * 2.0 ** -7) * np.exp2(-rng.integers(0, 7, (N, 8, 16, C, 4)).astype(np.float64)) * rng.choice([-1.0, 1.0], (N, 8, 16, C, 4))
    n = 2 * rng.integers(4, 8, (N, 8, 7, C)) + 1
    c = rng.choice([-1.0, 1.0], (N, 8, 7, C)) * 2.0 ** -8
    x[:, :, 0, :, 0] = 1.96875 * 2.0 ** 8 * rng.choice([-1.0, 1.0], (N, 8, 1))
    x[:, :, 1:8, :, 0] = c * n
    x[:, :, 8:15, :, 0] = -8.0 * c
    x[:, :, 8:15, :, 1] = -c * (n - 8 + rng.choice([-0.5, 0.5], (N, 8, 7, C)))
    u = d["u"].reshape(N, 128, 128, 4)
    for l in range(7):
        u[:, :, l::16] = 0
        for h in range(0, 128, 16):
            u[:, h + 1 + l, h + l, 0] = 1.0
            u[:, h + 8 + l, h + l, :2] = 1.0
    w = layers(rng)
    w[:, :, :, 0, :, :15] = 0
    w[:, :, :, 1, :, 8:15] = 0
    w[:, :, 0, :, :, :, 0] = 0
    return {"x": x.astype(np.float32).reshape(N, 128, 4 * C).astype(BF), "u": u.reshape(N, 128, 512), "v": d["v"], **lists(rng), **weights(rng, w)}
def setup_inputs_ends(rng):
    d = numbers_of(rng)
    o = rng.permutation(N) % 4
    j = np.arange(C)
    s = rng.choice([-1.0, 1.0], (N, 128, C, 4))
    s[o == 0] = -1
    s[o == 1] = (1.0 - j % 2 * 2.0)[:, None]
    x = s * (0.83 + 0.02 * rng.random((N, 128, C, 4))) * 2.0 ** 30
    x[o == 3] = -(1.0 + 0.125 * rng.integers(0, 8, (N, 128, C, 4))[o == 3]) * 2.0 ** -30
    size = np.where(o == 3, 2.0 ** -30, 2.0 ** 30)
    a = rng.permuted(np.tile(np.arange(8) % 2 * 2.0 - 1.0, (N, 7, 1)), axis=2).transpose(0, 2, 1) * size[:, None, None]
    for r in range(N): a[r, rng.permutation(8)[:2]] = 0
    u = d["u"].reshape(N, 128, 8, 16, 4)
    u[:, :, :, :7] = a.astype(np.float32).astype(BF)[:, None, :, :, None]
    v = rng.choice([-1.0, 1.0], (N, 128, 512)) * np.where(o % 2 == 0, 2.0 ** 30, 2.0 ** -30)[:, None, None]
    t = np.stack([j, (j + 2) % C, C - 1 - j, (j + 1) % C])
    k = rng.integers(0, 2, (N, 8, 2)) + 2 * (rng.permutation(8) < 4)[:, None]
    w = np.zeros((N, 128, 4, 128, 4), np.float32)
    i = np.arange(128)
    for b in range(4): w[:, i, b, i, b] = np.where(o == 3, 32.0, -1.0)[:, None]
    return {"x": x.astype(np.float32).reshape(N, 128, 4 * C).astype(BF), "u": u.reshape(N, 128, 512), "v": v.astype(np.float32).astype(BF), **stored(t[k]), **weights(rng, w.astype(BF))}
def setup_inputs_spread(rng):
    d = setup_inputs(rng)
    d["x"] = wide(rng, N, 128, 4 * C, cols=6)
    return d
def check_inputs(d):
    b = []
    for k in ("x", "u", "v"):
        a = np.abs(d[k].astype(np.float32))
        if not (np.isfinite(a).all() and ((a == 0) | (a >= 2.0 ** -30) & (a <= 2.0 ** 30)).all()): b.append("a value of " + k)
    none, least, most = [emit(mx_ref.quantize(np.full((128, 16), k, np.float32).astype(BF)))[1][0, 0] for k in (0.0, 2.0 ** -8, 2.0 ** 8)]
    for r in range(N):
        if not (np.sort(gentries(d["se"][r]).reshape(8, 2, C), axis=2) == np.arange(C)).all(): b.append("se: a list that is no permutation")
        if ((d["wc"][r] == 0x7F) | (d["wc"][r] == 0xFF)).any(): b.append("wc: a code that is no number")
        s = mx_ref.live(d["ws"][r])
        if ((s != none) & ((s < least) | (s > most))).any(): b.append("ws: a scale out of range")
    return b
def reference(x, u, v, se, wc, ws):
    qu = [mx_ref.quantize(u[r]) for r in range(N)]
    lay = [pk(wc[r], ws[r]) for r in range(N)]
    sec = [gentries(se[r]).reshape(8, 2, C) for r in range(N)]
    now = [x[r] for r in range(N)]
    g = np.arange(8)[:, None]
    for m in MASK:
        new, out = [], []
        for r in range(N):
            p = r ^ m
            bit = (mx_ref.matmul(qu[r], mx_ref.quantize(now[r])).reshape(8, 16, C)[:, :7] > 0).astype(np.int64)
            i = np.tile(np.arange(C), (8, 1))
            k = i
            for l in range(6):
                b = bit[g, l, i]
                i, k = sec[r][g, b, i], sec[p][g, 1 - b, k]
            end = bit[g, 6, k]
            turn = np.arange(C) ^ end ^ end[:, np.arange(C) ^ 1]
            new.append(np.stack([sec[p][g, 1 - b, turn[g, sec[r][:, b]]] for b in range(2)], axis=1))
            z = mx_ref.quantize(((gcols(now[r], i).astype(np.float32) + gcols(now[r], k).astype(np.float32)) * np.float32(0.5)).astype(BF))
            out.append(mx_ref.quantize(tile([mx_ref.matmul(pick(lay[r], np.arange(128 * b, 128 * b + 128)), z) * np.float32(0.03125) for b in range(4)])))
        now = [(now[r].astype(np.float32) + gcols(decode(out[r ^ m]).astype(BF), new[r][:, 0]).astype(np.float32)).astype(BF) for r in range(N)]
        sec = new
    y, so = np.zeros((N, 128, C), np.float32), np.zeros((N, 8, 2 * C), np.float32)
    oc, osc = np.zeros((N, 128, 4 * C), np.uint8), np.zeros((N, 16, C), np.uint8)
    for r in range(N):
        q = mx_ref.quantize(now[r])
        y[r] = mx_ref.matmul(mx_ref.quantize(v[r]), q)
        so[r] = sec[r].reshape(8, 2 * C)
        oc[r], osc[r] = emit(q)
    return {"y": y, "so": so, "oc": oc, "osc": osc}

@@ -1,0 +1,448 @@
+from concourse.bass import DstId, RemoteDMATransfer
+from concourse.mybir import dt, AluOpType as OP, ActivationFunctionType as AF
+
+C = 352
+MASK = [2, 4, 1]
+CH = 88
+BF, F32, I32, U16, U8, E4 = "bfloat16", "float32", "int32", "uint16", "uint8", "float8_e4m3fn_x4"
+SCRATCH = {
+    "sei": ("sbuf", [128, 44], I32), "ub": ("sbuf", [128, 512], BF), "vb": ("sbuf", [128, 512], BF),
+    "wq": ("sbuf", [128, 512], E4), "wp": ("sbuf", [128, 512], U8),
+    "uq": ("sbuf", [128, 128], E4), "us": ("sbuf", [128, 128], U8), "vq": ("sbuf", [128, 128], E4), "vs": ("sbuf", [128, 128], U8),
+    "u6q": ("sbuf", [128, 128], E4), "u6s": ("sbuf", [128, 128], U8),
+    "pc": ("sbuf", [128, 8], I32), "ci": ("sbuf", [128, 8], I32), "cf": ("sbuf", [128, 8], F32), "cg": ("sbuf", [128, 8], F32),
+    "par": ("sbuf", [128, 384], F32), "mk1": ("sbuf", [128, 384], F32), "mk2": ("sbuf", [128, 384], F32),
+    "j16": ("sbuf", [128, 704], F32), "j4": ("sbuf", [128, C], F32), "w6": ("sbuf", [128, 704], F32),
+    "m16": ("sbuf", [128, 704], BF), "r16": ("sbuf", [128, 704], BF), "m4": ("sbuf", [128, C], BF), "r4": ("sbuf", [128, C], BF),
+    "clf": ("sbuf", [128, 22], F32), "cl": ("sbuf", [128, 22], I32), "lpf": ("sbuf", [128, 44], F32), "lph": ("sbuf", [128, 44], U16),
+    "u6f": ("sbuf", [128, 8], F32), "u6l": ("sbuf", [128, 8], U16),
+    "one": ("sbuf", [128, 512], BF), "eb": ("sbuf", [128, 2048], BF), "eq": ("sbuf", [128, 512], E4), "es": ("sbuf", [128, 512], U8),
+    "xq": ("sbuf", [128, 384], E4), "xs": ("sbuf", [128, 384], U8), "xh": ("sbuf", [128, 1408], BF), "b6": ("sbuf", [128, C], BF),
+    "kk": ("sbuf", [128, 736], BF), "tt": ("sbuf", [128, 736], BF), "fm": ("sbuf", [128, 264], F32), "fb": ("sbuf", [128, 264], F32),
+    "fo": ("sbuf", [128, 264], F32), "fl": ("sbuf", [128, 132], U16), "tl": ("sbuf", [128, 44], U16), "sd": ("sbuf", [128, 22], F32),
+    "wm": ("sbuf", [128, C], F32), "wsn": ("sbuf", [128, C], F32), "vi": ("sbuf", [128, 22], I32), "vk": ("sbuf", [128, 66], I32),
+    "im": ("sbuf", [128, C], F32), "isn": ("sbuf", [128, C], F32), "ii": ("sbuf", [128, 88], I32), "ij": ("sbuf", [128, 88], I32),
+    "ix": ("sbuf", [128, 88], U16),
+    "wf": ("sbuf", [128, 704], BF), "pl": ("sbuf", [128, 44], BF), "ll": ("sbuf", [128, 88], U16), "pw": ("sbuf", [128, 704], BF),
+    "dp": ("sbuf", [128, C], F32), "s2": ("sbuf", [128, 2048], BF), "km": ("sbuf", [128, C], BF), "ksn": ("sbuf", [128, C], BF),
+    "ki": ("sbuf", [128, 22], I32), "k1": ("sbuf", [128, 22], U16), "k2": ("sbuf", [128, 22], U16), "k3": ("sbuf", [128, 22], U16),
+    "k6": ("sbuf", [128, 22], U16), "kx": ("sbuf", [128, 88], U16),
+    "en": ("sbuf", [128, C], BF), "dd": ("sbuf", [128, 176], BF), "xx": ("sbuf", [128, C], F32), "pt": ("sbuf", [128, 704], BF),
+    "tm": ("sbuf", [128, 704], BF), "ts": ("sbuf", [128, 704], BF), "t4": ("sbuf", [128, C], BF), "t4s": ("sbuf", [128, C], BF),
+    "tx": ("sbuf", [128, 88], U16), "tw": ("sbuf", [128, 704], F32),
+    "gi": ("sbuf", [128, 1408], BF), "z": ("sbuf", [128, 1408], BF), "zq": ("sbuf", [128, C], E4), "zs": ("sbuf", [128, C], U8),
+    "hb": ("sbuf", [128, 1408], BF), "dw": ("sbuf", [128, 1408], BF), "yb": ("sbuf", [128, C], F32),
+    "pa": ("psum", [128, 2048], F32), "pb": ("psum", [128, 2048], F32),
+}
+for _r in range(4):
+    SCRATCH["xp%d" % _r] = ("sbuf", [128, 1536], BF)
+for _r in range(3):
+    SCRATCH["sl%d" % _r] = ("sbuf", [128, 44], BF)
+    SCRATCH["lh%d" % _r] = ("sbuf", [128, 44], BF)
+    SCRATCH["ld%d" % _r] = ("dram", [128, 44], BF)
+    SCRATCH["hq%d" % _r] = ("sbuf", [128, C], E4)
+    SCRATCH["hs%d" % _r] = ("sbuf", [128, C], U8)
+    SCRATCH["fq%d" % _r] = ("sbuf", [128, CH], E4)
+    SCRATCH["fs%d" % _r] = ("sbuf", [128, CH], U8)
+    SCRATCH["dq%d" % _r] = ("sbuf", [128, C], E4)
+    SCRATCH["ds%d" % _r] = ("sbuf", [128, C], U8)
+SEMAPHORES = ["sv", "sa", "sp", "sg", "ls"] + ["d_" + n for n in ("se", "x", "u", "w", "wp", "v", "y", "oc", "so")]
+for _r in range(3):
+    SEMAPHORES += [n + str(_r) for n in ("hl", "hc", "hp", "la", "ca", "cb", "rp")]
+
+
+def route(topo, core, dst):
+    ok = [h for h in topo.cores_of(core) if h != core and topo.may_write(h, dst)]
+    near = [h for h in ok if topo.die(h) == topo.die(core)]
+    far = [h for h in ok if topo.die(h) != topo.die(core)]
+    return [near[0], far[0], near[1], far[1]]
+
+
+def bits(e):
+    return sum(1 << i for i in e)
+
+
+def hand_on(g, core, T, topo):
+    mine = [c for c in T.cores if c in topo.cores_of(core)]
+    sent = 0
+    for r in range(3):
+        for c in mine:
+            dst = T.cores[T.rank_of(c) ^ MASK[r]]
+            hs = route(topo, c, dst)
+            if core not in hs:
+                continue
+            i = hs.index(core)
+            rid, pid = topo.addr(dst, core)
+            e = topo.engines(core, dst)
+            n_in = len(topo.engines(c, core)) // 2
+            if i == 0:
+                g.wait_ge(T.sem["hl%d" % r], n_in)
+                g.remote_dma(T["ld%d" % r][:, :], T["lh%d" % r][:, :], T.sem["la%d" % r], T.sem.ls, pid, rid, bits(e))
+                sent += len(e)
+            arr = T.sem[("ca%d" if i < 2 else "cb%d") % r]
+            a = CH * i
+            g.wait_ge(T.sem["hc%d" % r], n_in)
+            g.remote_dma(T["dq%d" % r][:, a:a + CH].bitcast(dt.uint8), T["fq%d" % r][:, 0:CH].bitcast(dt.uint8), arr, T.sem.ls, pid, rid, bits(e))
+            g.wait_ge(T.sem["hp%d" % r], n_in)
+            g.remote_dma(T["ds%d" % r][:, a:a + CH], T["fs%d" % r][:, 0:CH], arr, T.sem.ls, pid, rid, bits(e))
+            sent += 2 * len(e)
+    if sent:
+        g.wait_ge(T.sem.ls, sent)
+
+
+def rank_program(g, core, T, topo):
+    rank = T.rank_of(core)
+    if rank is None:
+        hand_on(g, core, T, topo)
+        return
+    eng = {"v": g.vector, "a": g.scalar, "p": g.tensor, "g": g, "s": g.sync}
+    sem_of = {"v": "sv", "a": "sa", "p": "sp", "g": "sg"}
+    total, seen = {}, {}
+    last, readers = {}, {}
+
+    def need(q, r, w):
+        d = {}
+        for k in r:
+            t = last.get(k)
+            if t is not None:
+                d[t[0]] = max(d.get(t[0], 0), t[1])
+        for k in w:
+            for t in readers.get(k, []) + ([last[k]] if k in last else []):
+                if t[2] != q or t[0][0:2] == "d_":
+                    d[t[0]] = max(d.get(t[0], 0), t[1])
+        for s in d:
+            if seen.get((q, s), 0) < d[s]:
+                eng[q].wait_ge(T.sem[s], d[s])
+                seen[(q, s)] = d[s]
+
+    def mark(q, t, r, w):
+        for k in r:
+            readers[k] = [x for x in readers.get(k, []) if x[0] != t[0]] + [t]
+        for k in w:
+            last[k] = t
+            readers[k] = []
+
+    def op(q, r, w, f, *args, **kw):
+        r, w = r.split(), w.split()
+        need(q, r, w)
+        s = sem_of[q]
+        f(*args, **kw).then_inc(T.sem[s], 1)
+        total[s] = total.get(s, 0) + 1
+        mark(q, (s, total[s], q), r, w)
+
+    def dma(q, sem, r, w, out, in_):
+        r, w = r.split(), w.split()
+        need(q, r, w)
+        eng[q].dma_start(out, in_).then_inc(T.sem[sem], 16)
+        total[sem] = total.get(sem, 0) + 16
+        mark(q, (sem, total[sem], q), r, w)
+
+    V, A, P = g.vector, g.scalar, g.tensor
+
+    def ts(r, w, out, in0, s1, s2, o0, o1=None):
+        if o1 is None:
+            op("v", r, w, V.tensor_scalar, out, in0, s1, s2, o0)
+        else:
+            op("v", r, w, V.tensor_scalar, out, in0, s1, s2, o0, o1)
+
+    def tten(r, w, out, a, b, o):
+        op("v", r, w, V.tensor_tensor, out, a, b, o)
+
+    def cp(r, w, out, in_):
+        op("v", r, w, V.tensor_copy, out, in_)
+
+    def scan(r, w, out, d0, d1):
+        op("v", r, w, V.tensor_tensor_scan, out, d0, d1, 0.0, OP.mult, OP.add)
+
+    def act(r, w, out, in_, func=AF.Copy, **kw):
+        op("a", r, w, A.activation, out, in_, func, **kw)
+
+    def mm(r, w, out, wq, wsc, xq, xsc):
+        op("p", r, w, P.matmul_mx, out, wq, wsc, xq, xsc, True, True)
+
+    def arrived(key, sem, n):
+        total[sem] = n
+        last[key] = (sem, n, "r")
+        readers[key] = []
+
+    dma("s", "d_se", "", "sei", T.sei[:, :], T.se[:, :])
+    dma("s", "d_x", "", "xp0", T.xp0[:, 64:768], T.x[:, 0:704])
+    dma("a", "d_u", "", "ub", T.ub[:, :], T.u[:, :])
+    dma("a", "d_x", "", "xp0", T.xp0[:, 768:1472], T.x[:, 704:1408])
+    iota = g.iota
+    op("g", "", "pc", iota, T.pc[:, 0:1], [[0, 1]], 0, 1)
+    op("g", "", "u6f", iota, T.u6f[:, :], [[16, 8]], 6, 0, allow_small_or_imprecise_dtypes=True)
+    op("g", "", "par", iota, T.par[:, :], [[0, 12], [1, 2], [0, 16]], 0, 0, allow_small_or_imprecise_dtypes=True)
+    for r in range(4):
+        op("v", "", "pad%d" % r, V.memset, T["xp%d" % r][:, 0:64], 0.0)
+        op("v", "", "pad%d" % r, V.memset, T["xp%d" % r][:, 1472:1536], 0.0)
+    op("v", "", "one", V.memset, T.one[:, :], 1.0)
+    op("v", "", "s2", V.memset, T.s2[:, :], 0.0)
+    op("v", "", "fm", V.memset, T.fm[:, :], 0.0)
+    cp("u6f", "u6l", T.u6l[:, :], T.u6f[:, :])
+    ci, cf, cg = T.ci, T.cf, T.cg
+    ts("pc", "ci", ci[:, 0:1], T.pc[:, 0:1], 15, None, OP.bitwise_and)
+    ts("pc", "ci", ci[:, 1:2], T.pc[:, 0:1], 2, 3, OP.logical_shift_right, OP.bitwise_and)
+    ts("pc", "ci", ci[:, 2:3], T.pc[:, 0:1], 3, None, OP.bitwise_and)
+    ts("pc", "ci", ci[:, 3:4], T.pc[:, 0:1], 4, 1, OP.logical_shift_right, OP.bitwise_and)
+    cp("ci", "cf", cf[:, 0:4], ci[:, 0:4])
+    PR, PQ, P4, PH = cf[:, 0:1], cf[:, 1:2], cf[:, 2:3], cf[:, 3:4]
+    ts("sei", "sl0", T.sl0[:, 0:22], T.sei[:, 22:44], -176.0, None, OP.add)
+    ts("sei", "sl0", T.sl0[:, 22:44], T.sei[:, 0:22], -176.0, None, OP.add)
+
+    sent = [0]
+
+    def partner(r):
+        return T.cores[rank ^ MASK[r]]
+
+    def send_list(r):
+        h = route(topo, core, partner(r))[0]
+        rid, pid = topo.addr(h, core)
+        e = topo.engines(core, h)
+        e = e[:len(e) // 2]
+        need("g", ["sl%d" % r], [])
+        g.remote_dma(T["lh%d" % r][:, :], T["sl%d" % r][:, :], T.sem["hl%d" % r], T.sem.ls, pid, rid, bits(e))
+        sent[0] += len(e)
+
+    def send_half(r, h):
+        hs = route(topo, core, partner(r))[2 * h:2 * h + 2]
+        for codes in (True, False):
+            tr = []
+            for i, k in enumerate(hs):
+                rid, pid = topo.addr(k, core)
+                e = topo.engines(core, k)
+                n = len(e) // 2
+                a = CH * (2 * h + i)
+                if codes:
+                    s, d = T["hq%d" % r][:, a:a + CH].bitcast(dt.uint8), T["fq%d" % r][:, 0:CH].bitcast(dt.uint8)
+                else:
+                    s, d = T["hs%d" % r][:, a:a + CH], T["fs%d" % r][:, 0:CH]
+                tr.append(RemoteDMATransfer(dst_ids=[DstId(rid=rid, pnc=pid)], dma_engine_mask=bits(e[n * i:n * i + n]),
+                                            remote_sem=T.sem[("hc%d" if codes else "hp%d") % r], src=s, dst=d))
+                sent[0] += n
+            need("g", ["hq%d%d" % (r, h)], [])
+            g.remote_dma_fused(tr, local_sem=T.sem.ls)
+
+    send_list(0)
+    op("g", "", "clf", iota, T.clf[:, :], [[16, 22]], 0, 0, allow_small_or_imprecise_dtypes=True)
+    op("g", "", "lpf", iota, T.lpf[:, :], [[1, 44]], 0, 0, allow_small_or_imprecise_dtypes=True)
+    op("g", "", "w6", iota, T.w6[:, :], [[16384, 2], [1, C]], 0, 0, allow_small_or_imprecise_dtypes=True)
+    op("g", "", "j16", iota, T.j16[:, :], [[0, 44], [1, 16]], 0, 0, allow_small_or_imprecise_dtypes=True)
+    op("g", "", "j4", iota, T.j4[:, :], [[0, 88], [1, 4]], 0, 0, allow_small_or_imprecise_dtypes=True)
+    for b in range(4):
+        op("g", "one", "eb", g.affine_select, T.eb[:, 512 * b:512 * b + 512], T.one[:, :], [[-1, 512]], OP.is_equal, 0.0, b, 4)
+    ts("par cf", "mk1", T.mk1[:, :], T.par[:, :], PH, 1e25, OP.is_equal, OP.mult)
+    ts("par cf", "mk2", T.mk2[:, :], T.par[:, :], PH, 1e25, OP.not_equal, OP.mult)
+    op("v", "ub", "uq", V.quantize_mx, T.uq[:, :], T.us[:, :], T.ub[:, :])
+    cp("uq u6l", "u6", T.u6q[:, :].bitcast(dt.uint32), T.uq[:, :].bitcast(dt.uint32).indirect(T.u6l[:, 0:8]))
+    act("uq u6l", "u6s", T.u6s[:, :], T.us[:, :].indirect(T.u6l[:, 0:8]))
+    need("s", ["xp0"], [])
+    dma("s", "d_w", "", "wq", T.wq[:, :].bitcast(dt.uint8), T.wc[:, :])
+    dma("s", "d_wp", "", "wp", T.wp[:, :], T.ws[:, :])
+    dma("s", "d_v", "", "vb", T.vb[:, :], T.v[:, :])
+
+    def own_lists(r):
+        sl, k = T["sl%d" % r], "sl%d" % r
+        ts(k, "tl", T.tl[:, 0:22], sl[:, 0:22], 528.0, None, OP.add)
+        ts(k, "tl", T.tl[:, 22:44], sl[:, 22:44], 176.0, None, OP.add)
+        tten(k, "sd", T.sd[:, :], sl[:, 0:22], sl[:, 22:44], OP.subtract)
+        ts(k, "fb", T.fb[:, 1:44:2], sl[:, 22:44], 176.0, None, OP.add)
+        ts("sd", "fb", T.fb[:, 0:44:2], T.sd[:, :], 352.0, None, OP.add)
+        cp("fb", "fb", T.fb[:, 44:88], T.fb[:, 0:44])
+        cp("fb", "fb", T.fb[:, 88:176], T.fb[:, 0:88])
+        cp("fb", "fb", T.fb[:, 176:264], T.fb[:, 0:88])
+
+    def fetch(r):
+        arrived("ld%d" % r, "la%d" % r, len(topo.engines(route(topo, partner(r), core)[0], core)))
+        ld = T["ld%d" % r]
+        dma("s", "rp%d" % r, "ld%d" % r, "pl", T.pl[:, :], ld[:, :])
+        for i in range(16):
+            dma("s", "rp%d" % r, "ld%d" % r, "wf%d" % i, T.wf[i:128:16, :], ld[:, :])
+        for k in ["pl"] + ["wf%d" % i for i in range(16)]:
+            last[k] = ("rp%d" % r, total["rp%d" % r], "s")
+
+    WF = " ".join("wf%d" % i for i in range(16))
+
+    def tables(r):
+        for e in range(2):
+            ts("pl", "ll", T.ll[:, 44 * e:44 * e + 44], T.pl[:, :], 176.0 + 352.0 * e, None, OP.add)
+        act(WF + " lph", "pw", T.pw[:, :], T.wf[:, :].indirect(T.lph[:, :]))
+        for e in range(4):
+            o, a = T.s2[:, 512 * e:512 * e + C], T.pw[:, :].indirect(T.ll[:, 22 * e:22 * e + 22])
+            if r == 0 and e >= 2:
+                cp("pw ll", "s2", o, a)
+            else:
+                act("pw ll", "s2", o, a)
+
+    def bank(b, h):
+        return (T.pb if h else T.pa)[:, 512 * b:512 * b + 512], ("pb%d" if h else "pa%d") % b
+
+    def qx(r):
+        op("v", "xp%d pad%d" % (r, r), "xq", V.quantize_mx, T.xq[:, :], T.xs[:, :], T["xp%d" % r][:, :])
+
+    for r in range(3):
+        XP = T["xp%d" % r]
+        if r == 0:
+            own_lists(0)
+        qx(r)
+        mm("uq xq", "pb0", T.pb[:, 0:384], T.uq[:, :], T.us[:, :], T.xq[:, :], T.xs[:, :])
+        mm("u6 u6s xq", "pb1", T.pb[:, 512:512 + C], T.u6q[:, :], T.u6s[:, :], T.xq[:, 16:368], T.xs[:, 16:368])
+        act("xp%d" % r, "xh", T.xh[:, :], XP[:, 64:1472], scale=0.5)
+        act("pb1", "b6", T.b6[:, :], T.pb[:, 512:512 + C], AF.Sign, bias=-2.0 ** -93)
+        tten("pb0 mk1", "kk", T.kk[:, 0:352], T.pb[:, 16:368], T.mk1[:, 16:368], OP.is_gt)
+        tten("pb0 mk2", "kk", T.kk[:, 352:736], T.pb[:, 0:384], T.mk2[:, 0:384], OP.is_gt)
+        op("v", "kk", "tt", V.transpose, T.tt[:, :], T.kk[:, :])
+        for l in range(6):
+            a = 44 * l
+            tten("tt", "fm", T.fm[:, a + 1:a + 44:4], T.tt[:, l:352:32], T.tt[:, 368 + l:704:32], OP.add)
+            tten("tt", "fm", T.fm[:, a + 3:a + 44:4], T.tt[:, 384 + l:736:32], T.tt[:, 16 + l:352:32], OP.add)
+        scan("fm fb", "fo", T.fo[:, :], T.fm[:, :], T.fb[:, :])
+        cp("fo", "fl", T.fl[:, :], T.fo[:, 1:264:2])
+        if r == 0:
+            fetch(0)
+            ts("clf cf", "cl", T.cl[:, :], T.clf[:, :], PR, None, OP.add)
+            ts("cf", "cg", cg[:, 0:1], PR, 44.0, None, OP.mult)
+            ts("lpf cg", "lph", T.lph[:, :], T.lpf[:, :], cg[:, 0:1], None, OP.add)
+            ts("cf", "cg", cg[:, 1:2], P4, 704.0, None, OP.add)
+            ts("cf", "cg", cg[:, 2:3], P4, 352.0, 176.0, OP.mult, OP.add)
+        else:
+            tables(r)
+        W, key = T.w6, "w6"
+        for l in range(5, 0, -1):
+            N_, nk = (T.wv0, "wv0") if l % 2 else (T.wv1, "wv1")
+            off = T.fl[:, 22 * l:22 * l + 22]
+            rk = key if key == "w6" else key + "a " + key + "b"
+            cp(rk + " fl", nk + "a", N_[:, 0:352], W[:, :].indirect(off))
+            act(rk + " fl", nk + "b", N_[:, 352:704], W[:, :].indirect(off), AF.Identity, bias=float(512 << (l - 1)))
+            W, key = N_, nk
+            if r == 0:
+                if l == 5:
+                    ts("j16 cf", "m16", T.m16[:, 0:352], T.j16[:, 0:352], PR, None, OP.is_equal)
+                if l == 4:
+                    ts("j16", "r16", T.r16[:, 0:352], T.j16[:, 0:352], 0.0, None, OP.not_equal)
+                if l == 3:
+                    ts("j4 cf", "m4", T.m4[:, :], T.j4[:, :], PQ, None, OP.is_equal)
+                if l == 2:
+                    ts("j4", "r4", T.r4[:, :], T.j4[:, :], 0.0, None, OP.not_equal)
+        rk = key + "a " + key + "b fl"
+        win = W[:, :].indirect(T.fl[:, 0:22])
+        tten(rk + " m16", "wm", T.wm[:, :], win, T.m16[:, 0:352], OP.mult)
+        scan("wm r16", "wsn", T.wsn[:, :], T.r16[:, 0:352], T.wm[:, :])
+        cp("wsn", "vi", T.vi[:, :], T.wsn[:, 15:352:16])
+        ts("vi", "vk", T.vk[:, 0:22], T.vi[:, :], 0x600, None, OP.bitwise_and)
+        tten("vk cl", "ki", T.ki[:, :], T.vk[:, 0:22], T.cl[:, :], OP.add)
+        cp("ki", "k1", T.k1[:, :], T.ki[:, :])
+        ts("vi", "vk2", T.vk[:, 22:44], T.vi[:, :], 2, 0x600, OP.logical_shift_right, OP.bitwise_and)
+        ts("vi", "vk3", T.vk[:, 44:66], T.vi[:, :], 4, 0x600, OP.logical_shift_right, OP.bitwise_and)
+        tten(rk + " m4", "im", T.im[:, :], win, T.m4[:, :], OP.mult)
+        scan("im r4", "isn", T.isn[:, :], T.r4[:, :], T.im[:, :])
+        cp("isn", "ii", T.ii[:, :], T.isn[:, 3:352:4])
+        ts("ii", "ij", T.ij[:, :], T.ii[:, :], 511, None, OP.bitwise_and)
+        ts("ij cf", "ix", T.ix[:, :], T.ij[:, :], 4.0, P4, OP.mult, OP.add)
+        if r == 0:
+            tables(0)
+        for h in range(2):
+            act("xh ix", "gi%d" % h, T.gi[:, 704 * h:704 * h + 704], T.xh[:, :].indirect(T.ix[:, 44 * h:44 * h + 44]))
+        for j in (1, 2):
+            tten("s2 k%d m16" % j, "km", T.km[:, :], T.s2[:, :].indirect(T["k%d" % j][:, :]), T.m16[:, 0:352], OP.mult)
+            scan("km r16", "ksn", T.ksn[:, :], T.r16[:, 0:352], T.km[:, :])
+            tten("ksn vk%d" % (j + 1), "ki", T.ki[:, :], T.ksn[:, 15:352:16], T.vk[:, 22 * j:22 * j + 22], OP.add)
+            ts("ki", "k%d" % (j + 1), T["k%d" % (j + 1)][:, :], T.ki[:, :], 176.0, None, OP.add)
+        tten("s2 k3 m4", "km", T.km[:, :], T.s2[:, :].indirect(T.k3[:, :]), T.m4[:, :], OP.mult)
+        scan("km r4", "ksn", T.ksn[:, :], T.r4[:, :], T.km[:, :])
+        ts("ksn cg", "kx", T.kx[:, :], T.ksn[:, 3:352:4], 4.0, cg[:, 1:2], OP.mult, OP.add)
+        def mosaic(h):
+            a = 704 * h
+            tten("xh kx gi%d" % h, "z%d" % h, T.z[:, a:a + 704], T.xh[:, :].indirect(T.kx[:, 44 * h:44 * h + 44]), T.gi[:, a:a + 704], OP.add)
+            op("v", "z%d" % h, "zq%d" % h, V.quantize_mx, T.zq[:, 176 * h:176 * h + 176], T.zs[:, 176 * h:176 * h + 176], T.z[:, a:a + 704])
+            for b in range(4):
+                o, k = bank(b, h)
+                mm("wq wp zq%d" % h, k, o[:, 0:176] if False else (T.pb if h else T.pa)[:, 512 * b:512 * b + 176], T.wq[:, 128 * b:128 * b + 128], T.wp[:, 128 * b:128 * b + 128], T.zq[:, 176 * h:176 * h + 176], T.zs[:, 176 * h:176 * h + 176])
+
+        def hcast(h, b, q):
+            i = (T.pb if h else T.pa)[:, 512 * b:512 * b + 176]
+            o = T.hb[:, 704 * h + b:704 * h + 704:4]
+            k = ("pb%d" if h else "pa%d") % b
+            if q == "a":
+                act(k, "hb%d%d" % (h, b), o, i, scale=0.03125)
+            else:
+                ts(k, "hb%d%d" % (h, b), o, i, 0.03125, None, OP.mult)
+
+        def qh(h):
+            op("v", " ".join("hb%d%d" % (h, b) for b in range(4)), "hq%d%d" % (r, h), V.quantize_mx, T["hq%d" % r][:, 176 * h:176 * h + 176],
+               T["hs%d" % r][:, 176 * h:176 * h + 176], T.hb[:, 704 * h:704 * h + 704])
+            send_half(r, h)
+
+        mosaic(0)
+        for b in range(4):
+            hcast(0, b, "a")
+        mosaic(1)
+        qh(0)
+        tten("s2 k3 m16", "km", T.km[:, :], T.s2[:, :].indirect(T.k3[:, :]), T.m16[:, 0:352], OP.mult)
+        hcast(1, 0, "a")
+        hcast(1, 2, "v")
+        hcast(1, 1, "a")
+        hcast(1, 3, "v")
+        qh(1)
+        scan("km r16", "ksn", T.ksn[:, :], T.r16[:, 0:352], T.km[:, :])
+        ts("ksn", "k6", T.k6[:, :], T.ksn[:, 15:352:16], 176.0, None, OP.add)
+        act("b6 k6", "en", T.en[:, :], T.b6[:, :].indirect(T.k6[:, :]))
+        if r == 0:
+            ts("j16 cf", "m16", T.m16[:, 352:704], T.j16[:, 352:704], PR, None, OP.is_equal)
+            ts("j16", "r16", T.r16[:, 352:704], T.j16[:, 352:704], 0.0, None, OP.not_equal)
+        tten("pw", "dp", T.dp[:, :], T.pw[:, 1:704:2], T.pw[:, 0:704:2], OP.subtract)
+        tten("en", "dd", T.dd[:, :], T.en[:, 0:352:2], T.en[:, 1:352:2], OP.not_equal)
+        for b in range(2):
+            tten("dd dp", "xx", T.xx[:, 176 * b:176 * b + 176], T.dp[:, 176 * b:176 * b + 176], T.dd[:, :], OP.mult)
+        tten("pw xx", "pt", T.pt[:, 0:704:2], T.pw[:, 0:704:2], T.xx[:, :], OP.add)
+        tten("pw xx", "pt", T.pt[:, 1:704:2], T.pw[:, 1:704:2], T.xx[:, :], OP.subtract)
+        if r < 2:
+            tten("pt tl m16", "tm", T.tm[:, :], T.pt[:, :].indirect(T.tl[:, :]), T.m16[:, :], OP.mult)
+            scan("tm r16", "ts", T.ts[:, :], T.r16[:, :], T.tm[:, :])
+            cp("ts", "sl%d" % (r + 1), T["sl%d" % (r + 1)][:, :], T.ts[:, 15:704:16])
+            send_list(r + 1)
+            fetch(r + 1)
+        tten("pt tl m4", "t4", T.t4[:, :], T.pt[:, :].indirect(T.tl[:, 22:44]), T.m4[:, :], OP.mult)
+        scan("t4 r4", "t4s", T.t4s[:, :], T.r4[:, :], T.t4[:, :])
+        ts("t4s cg", "tx", T.tx[:, :], T.t4s[:, 3:352:4], cg[:, 2:3], None, OP.add)
+        if r < 2:
+            own_lists(r + 1)
+        if r == 0:
+            op("v", "eb", "eq", V.quantize_mx, T.eq[:, :], T.es[:, :], T.eb[:, :])
+            op("v", "vb", "vq", V.quantize_mx, T.vq[:, :], T.vs[:, :], T.vb[:, :])
+        hp = route(topo, partner(r), core)
+        for h in range(2):
+            arrived("dq%d%d" % (r, h), ("ca%d" if h == 0 else "cb%d") % r, sum(2 * len(topo.engines(k, core)) for k in hp[2 * h:2 * h + 2]))
+            for b in range(4):
+                ps = (T.pb if h else T.pa)[:, 512 * b:512 * b + 176]
+                k = ("pb%d" if h else "pa%d") % b
+                mm("eq dq%d%d" % (r, h), k, ps, T.eq[:, 128 * b:128 * b + 128], T.es[:, 128 * b:128 * b + 128],
+                   T["dq%d" % r][:, 176 * h:176 * h + 176], T["ds%d" % r][:, 176 * h:176 * h + 176])
+            for b in range(4):
+                ps = (T.pb if h else T.pa)[:, 512 * b:512 * b + 176]
+                k = ("pb%d" if h else "pa%d") % b
+                o = T.dw[:, 352 * b + 176 * h:352 * b + 176 * h + 176]
+                if h == 0 or b < 2:
+                    act(k, "dw%d%d" % (h, b), o, ps)
+                else:
+                    cp(k, "dw%d%d" % (h, b), o, ps)
+        tten("tx xp%d " % r + " ".join("dw%d%d" % (h, b) for h in range(2) for b in range(4)), "xp%d" % (r + 1),
+             T["xp%d" % (r + 1)][:, 64:1472], T.dw[:, :].indirect(T.tx[:, :]), XP[:, 64:1472], OP.add)
+
+    act("pt tl", "tw", T.tw[:, :], T.pt[:, :].indirect(T.tl[:, :]), AF.Identity, bias=176.0)
+    dma("s", "d_so", "tw", "so", T.so[:, 0:352], T.tw[0:128:16, 352:704])
+    dma("s", "d_so", "tw", "so2", T.so[:, 352:704], T.tw[0:128:16, 0:352])
+    qx(3)
+    dma("s", "d_oc", "xq", "oc", T.oc[:, :], T.xq[:, 16:368].bitcast(dt.uint8))
+    for k in range(4):
+        dma("s", "d_oc", "xq", "osc%d" % k, T.osc[4 * k:4 * k + 4, :], T.xs[32 * k:32 * k + 4, 16:368])
+    mm("vq xq", "pa0", T.pa[:, 0:C], T.vq[:, :], T.vs[:, :], T.xq[:, 16:368], T.xs[:, 16:368])
+    cp("pa0", "yb", T.yb[:, :], T.pa[:, 0:C])
+    dma("s", "d_y", "yb", "y", T.y[:, :], T.yb[:, :])
+    total["ls"] = sent[0]
+    for s in total:
+        g.wait_ge(T.sem[s], total[s])
+
+
+SCRATCH["wv0"] = ("sbuf", [128, 704], F32)
+SCRATCH["wv1"] = ("sbuf", [128, 704], F32)

@@ -3,7 +3,7 @@ from concourse.mybir import dt, AluOpType as OP, ActivationFunctionType as AF
 
 C = 352
 MASK = [2, 4, 1]
-CH = 88
+HALF = [(0, 192), (192, 160)]
 BF, F32, I32, U16, U8, E4 = "bfloat16", "float32", "int32", "uint16", "uint8", "float8_e4m3fn_x4"
 SCRATCH = {
     "sei": ("sbuf", [128, 44], I32), "ub": ("sbuf", [128, 512], BF), "vb": ("sbuf", [128, 512], BF),
@@ -12,24 +12,23 @@ SCRATCH = {
     "u6q": ("sbuf", [128, 128], E4), "u6s": ("sbuf", [128, 128], U8),
     "pc": ("sbuf", [128, 8], I32), "ci": ("sbuf", [128, 8], I32), "cf": ("sbuf", [128, 8], F32), "cg": ("sbuf", [128, 8], F32),
     "par": ("sbuf", [128, 384], F32), "mk1": ("sbuf", [128, 384], F32), "mk2": ("sbuf", [128, 384], F32),
-    "j16": ("sbuf", [128, 704], F32), "j4": ("sbuf", [128, C], F32), "w6": ("sbuf", [128, 704], F32),
-    "m16": ("sbuf", [128, 704], BF), "r16": ("sbuf", [128, 704], BF), "m4": ("sbuf", [128, C], BF), "r4": ("sbuf", [128, C], BF),
+    "j16": ("sbuf", [128, C], F32), "w6": ("sbuf", [128, 704], F32), "m16": ("sbuf", [128, 704], BF), "r16": ("sbuf", [128, 704], BF),
     "clf": ("sbuf", [128, 22], F32), "cl": ("sbuf", [128, 22], I32), "lpf": ("sbuf", [128, 44], F32), "lph": ("sbuf", [128, 44], U16),
     "u6f": ("sbuf", [128, 8], F32), "u6l": ("sbuf", [128, 8], U16),
     "one": ("sbuf", [128, 512], BF), "eb": ("sbuf", [128, 2048], BF), "eq": ("sbuf", [128, 512], E4), "es": ("sbuf", [128, 512], U8),
     "xq": ("sbuf", [128, 384], E4), "xs": ("sbuf", [128, 384], U8), "xh": ("sbuf", [128, 1408], BF), "b6": ("sbuf", [128, C], BF),
     "kk": ("sbuf", [128, 736], BF), "tt": ("sbuf", [128, 736], BF), "fm": ("sbuf", [128, 264], F32), "fb": ("sbuf", [128, 264], F32),
-    "fo": ("sbuf", [128, 264], F32), "fl": ("sbuf", [128, 132], U16), "tl": ("sbuf", [128, 44], U16), "sd": ("sbuf", [128, 22], F32),
-    "wm": ("sbuf", [128, C], F32), "wsn": ("sbuf", [128, C], F32), "vi": ("sbuf", [128, 22], I32), "vk": ("sbuf", [128, 66], I32),
-    "im": ("sbuf", [128, C], F32), "isn": ("sbuf", [128, C], F32), "ii": ("sbuf", [128, 88], I32), "ij": ("sbuf", [128, 88], I32),
-    "ix": ("sbuf", [128, 88], U16),
+    "fo": ("sbuf", [128, 264], F32), "fl": ("sbuf", [128, 132], U16), "sd": ("sbuf", [128, 22], F32),
+    "wv0": ("sbuf", [128, 704], F32), "wv1": ("sbuf", [128, 704], F32),
+    "wm": ("sbuf", [128, C], F32), "wsn": ("sbuf", [128, C], F32), "vi": ("sbuf", [128, 22], I32), "vk": ("sbuf", [128, 88], I32),
+    "il": ("sbuf", [128, 22], U16),
     "wf": ("sbuf", [128, 704], BF), "pl": ("sbuf", [128, 44], BF), "ll": ("sbuf", [128, 88], U16), "pw": ("sbuf", [128, 704], BF),
-    "dp": ("sbuf", [128, C], F32), "s2": ("sbuf", [128, 2048], BF), "km": ("sbuf", [128, C], BF), "ksn": ("sbuf", [128, C], BF),
+    "s2": ("sbuf", [128, 2048], BF), "km": ("sbuf", [128, C], BF), "ksn": ("sbuf", [128, C], BF),
     "ki": ("sbuf", [128, 22], I32), "k1": ("sbuf", [128, 22], U16), "k2": ("sbuf", [128, 22], U16), "k3": ("sbuf", [128, 22], U16),
-    "k6": ("sbuf", [128, 22], U16), "kx": ("sbuf", [128, 88], U16),
-    "en": ("sbuf", [128, C], BF), "dd": ("sbuf", [128, 176], BF), "xx": ("sbuf", [128, C], F32), "pt": ("sbuf", [128, 704], BF),
-    "tm": ("sbuf", [128, 704], BF), "ts": ("sbuf", [128, 704], BF), "t4": ("sbuf", [128, C], BF), "t4s": ("sbuf", [128, C], BF),
-    "tx": ("sbuf", [128, 88], U16), "tw": ("sbuf", [128, 704], F32),
+    "k6": ("sbuf", [128, 22], U16),
+    "sn": ("sbuf", [128, 44], U16), "tf": ("sbuf", [128, 44], F32), "tg": ("sbuf", [128, 44], F32), "tl": ("sbuf", [128, 44], U16),
+    "en": ("sbuf", [128, C], BF), "dd": ("sbuf", [128, C], BF), "tm": ("sbuf", [128, 704], BF), "ts": ("sbuf", [128, 704], BF),
+    "tx": ("sbuf", [128, 22], U16), "tw": ("sbuf", [128, 704], F32),
     "gi": ("sbuf", [128, 1408], BF), "z": ("sbuf", [128, 1408], BF), "zq": ("sbuf", [128, C], E4), "zs": ("sbuf", [128, C], U8),
     "hb": ("sbuf", [128, 1408], BF), "dw": ("sbuf", [128, 1408], BF), "yb": ("sbuf", [128, C], F32),
     "pa": ("psum", [128, 2048], F32), "pb": ("psum", [128, 2048], F32),
@@ -42,11 +41,11 @@ for _r in range(3):
     SCRATCH["ld%d" % _r] = ("dram", [128, 44], BF)
     SCRATCH["hq%d" % _r] = ("sbuf", [128, C], E4)
     SCRATCH["hs%d" % _r] = ("sbuf", [128, C], U8)
-    SCRATCH["fq%d" % _r] = ("sbuf", [128, CH], E4)
-    SCRATCH["fs%d" % _r] = ("sbuf", [128, CH], U8)
+    SCRATCH["fq%d" % _r] = ("sbuf", [128, 96], E4)
+    SCRATCH["fs%d" % _r] = ("sbuf", [128, 96], U8)
     SCRATCH["dq%d" % _r] = ("sbuf", [128, C], E4)
     SCRATCH["ds%d" % _r] = ("sbuf", [128, C], U8)
-SEMAPHORES = ["sv", "sa", "sp", "sg", "ls"] + ["d_" + n for n in ("se", "x", "u", "w", "wp", "v", "y", "oc", "so")]
+SEMAPHORES = ["sv", "sa", "sp", "sg", "ls"] + ["d_" + n for n in ("se", "x", "x2", "u", "w", "wp", "v", "y", "oc", "so")]
 for _r in range(3):
     SEMAPHORES += [n + str(_r) for n in ("hl", "hc", "hp", "la", "ca", "cb", "rp")]
 
@@ -56,6 +55,11 @@ def route(topo, core, dst):
     near = [h for h in ok if topo.die(h) == topo.die(core)]
     far = [h for h in ok if topo.die(h) != topo.die(core)]
     return [near[0], far[0], near[1], far[1]]
+
+
+def chunk(i):
+    a, n = HALF[i // 2]
+    return a + n // 2 * (i % 2), n // 2
 
 
 def bits(e):
@@ -80,11 +84,11 @@ def hand_on(g, core, T, topo):
                 g.remote_dma(T["ld%d" % r][:, :], T["lh%d" % r][:, :], T.sem["la%d" % r], T.sem.ls, pid, rid, bits(e))
                 sent += len(e)
             arr = T.sem[("ca%d" if i < 2 else "cb%d") % r]
-            a = CH * i
+            a, n = chunk(i)
             g.wait_ge(T.sem["hc%d" % r], n_in)
-            g.remote_dma(T["dq%d" % r][:, a:a + CH].bitcast(dt.uint8), T["fq%d" % r][:, 0:CH].bitcast(dt.uint8), arr, T.sem.ls, pid, rid, bits(e))
+            g.remote_dma(T["dq%d" % r][:, a:a + n].bitcast(dt.uint8), T["fq%d" % r][:, 0:n].bitcast(dt.uint8), arr, T.sem.ls, pid, rid, bits(e))
             g.wait_ge(T.sem["hp%d" % r], n_in)
-            g.remote_dma(T["ds%d" % r][:, a:a + CH], T["fs%d" % r][:, 0:CH], arr, T.sem.ls, pid, rid, bits(e))
+            g.remote_dma(T["ds%d" % r][:, a:a + n], T["fs%d" % r][:, 0:n], arr, T.sem.ls, pid, rid, bits(e))
             sent += 2 * len(e)
     if sent:
         g.wait_ge(T.sem.ls, sent)
@@ -115,7 +119,7 @@ def rank_program(g, core, T, topo):
                 eng[q].wait_ge(T.sem[s], d[s])
                 seen[(q, s)] = d[s]
 
-    def mark(q, t, r, w):
+    def mark(t, r, w):
         for k in r:
             readers[k] = [x for x in readers.get(k, []) if x[0] != t[0]] + [t]
         for k in w:
@@ -128,14 +132,14 @@ def rank_program(g, core, T, topo):
         s = sem_of[q]
         f(*args, **kw).then_inc(T.sem[s], 1)
         total[s] = total.get(s, 0) + 1
-        mark(q, (s, total[s], q), r, w)
+        mark((s, total[s], q), r, w)
 
     def dma(q, sem, r, w, out, in_):
         r, w = r.split(), w.split()
         need(q, r, w)
         eng[q].dma_start(out, in_).then_inc(T.sem[sem], 16)
         total[sem] = total.get(sem, 0) + 16
-        mark(q, (sem, total[sem], q), r, w)
+        mark((sem, total[sem], q), r, w)
 
     V, A, P = g.vector, g.scalar, g.tensor
 
@@ -166,27 +170,32 @@ def rank_program(g, core, T, topo):
         readers[key] = []
 
     dma("s", "d_se", "", "sei", T.sei[:, :], T.se[:, :])
-    dma("s", "d_x", "", "xp0", T.xp0[:, 64:768], T.x[:, 0:704])
+    dma("s", "d_x", "", "xp00", T.xp0[:, 64:768], T.x[:, 0:704])
     dma("a", "d_u", "", "ub", T.ub[:, :], T.u[:, :])
-    dma("a", "d_x", "", "xp0", T.xp0[:, 768:1472], T.x[:, 704:1408])
-    iota = g.iota
-    op("g", "", "pc", iota, T.pc[:, 0:1], [[0, 1]], 0, 1)
-    op("g", "", "u6f", iota, T.u6f[:, :], [[16, 8]], 6, 0, allow_small_or_imprecise_dtypes=True)
-    op("g", "", "par", iota, T.par[:, :], [[0, 12], [1, 2], [0, 16]], 0, 0, allow_small_or_imprecise_dtypes=True)
+    dma("a", "d_x2", "", "xp01", T.xp0[:, 768:1472], T.x[:, 704:1408])
+
+    def iota(k, out, pattern, base, cm):
+        op("g", "", k, g.iota, out, pattern, base, cm, allow_small_or_imprecise_dtypes=True)
+
+    op("g", "", "pc", g.iota, T.pc[:, 0:1], [[0, 1]], 0, 1)
+    iota("u6f", T.u6f[:, :], [[16, 8]], 6, 0)
+    iota("par", T.par[:, :], [[0, 12], [1, 2], [0, 16]], 0, 0)
+    iota("j16", T.j16[:, :], [[0, 22], [1, 16]], 0, 0)
     for r in range(4):
         op("v", "", "pad%d" % r, V.memset, T["xp%d" % r][:, 0:64], 0.0)
         op("v", "", "pad%d" % r, V.memset, T["xp%d" % r][:, 1472:1536], 0.0)
     op("v", "", "one", V.memset, T.one[:, :], 1.0)
-    op("v", "", "s2", V.memset, T.s2[:, :], 0.0)
+    for e in range(4):
+        op("v", "", "s2g", V.memset, T.s2[:, 512 * e + C:512 * e + 512], 0.0)
+    op("v", "", "r16o", V.memset, T.r16[:, :], 1.0)
+    op("v", "r16o", "r16", V.memset, T.r16[:, 0:704:16], 0.0)
     op("v", "", "fm", V.memset, T.fm[:, :], 0.0)
-    cp("u6f", "u6l", T.u6l[:, :], T.u6f[:, :])
     ci, cf, cg = T.ci, T.cf, T.cg
     ts("pc", "ci", ci[:, 0:1], T.pc[:, 0:1], 15, None, OP.bitwise_and)
-    ts("pc", "ci", ci[:, 1:2], T.pc[:, 0:1], 2, 3, OP.logical_shift_right, OP.bitwise_and)
-    ts("pc", "ci", ci[:, 2:3], T.pc[:, 0:1], 3, None, OP.bitwise_and)
-    ts("pc", "ci", ci[:, 3:4], T.pc[:, 0:1], 4, 1, OP.logical_shift_right, OP.bitwise_and)
-    cp("ci", "cf", cf[:, 0:4], ci[:, 0:4])
-    PR, PQ, P4, PH = cf[:, 0:1], cf[:, 1:2], cf[:, 2:3], cf[:, 3:4]
+    ts("pc", "ci", ci[:, 1:2], T.pc[:, 0:1], 4, 1, OP.logical_shift_right, OP.bitwise_and)
+    cp("u6f", "u6l", T.u6l[:, :], T.u6f[:, :])
+    cp("ci", "cf", cf[:, 0:2], ci[:, 0:2])
+    PR, PH = cf[:, 0:1], cf[:, 1:2]
     ts("sei", "sl0", T.sl0[:, 0:22], T.sei[:, 22:44], -176.0, None, OP.add)
     ts("sei", "sl0", T.sl0[:, 22:44], T.sei[:, 0:22], -176.0, None, OP.add)
 
@@ -212,11 +221,11 @@ def rank_program(g, core, T, topo):
                 rid, pid = topo.addr(k, core)
                 e = topo.engines(core, k)
                 n = len(e) // 2
-                a = CH * (2 * h + i)
+                a, m = chunk(2 * h + i)
                 if codes:
-                    s, d = T["hq%d" % r][:, a:a + CH].bitcast(dt.uint8), T["fq%d" % r][:, 0:CH].bitcast(dt.uint8)
+                    s, d = T["hq%d" % r][:, a:a + m].bitcast(dt.uint8), T["fq%d" % r][:, 0:m].bitcast(dt.uint8)
                 else:
-                    s, d = T["hs%d" % r][:, a:a + CH], T["fs%d" % r][:, 0:CH]
+                    s, d = T["hs%d" % r][:, a:a + m], T["fs%d" % r][:, 0:m]
                 tr.append(RemoteDMATransfer(dst_ids=[DstId(rid=rid, pnc=pid)], dma_engine_mask=bits(e[n * i:n * i + n]),
                                             remote_sem=T.sem[("hc%d" if codes else "hp%d") % r], src=s, dst=d))
                 sent[0] += n
@@ -224,11 +233,9 @@ def rank_program(g, core, T, topo):
             g.remote_dma_fused(tr, local_sem=T.sem.ls)
 
     send_list(0)
-    op("g", "", "clf", iota, T.clf[:, :], [[16, 22]], 0, 0, allow_small_or_imprecise_dtypes=True)
-    op("g", "", "lpf", iota, T.lpf[:, :], [[1, 44]], 0, 0, allow_small_or_imprecise_dtypes=True)
-    op("g", "", "w6", iota, T.w6[:, :], [[16384, 2], [1, C]], 0, 0, allow_small_or_imprecise_dtypes=True)
-    op("g", "", "j16", iota, T.j16[:, :], [[0, 44], [1, 16]], 0, 0, allow_small_or_imprecise_dtypes=True)
-    op("g", "", "j4", iota, T.j4[:, :], [[0, 88], [1, 4]], 0, 0, allow_small_or_imprecise_dtypes=True)
+    iota("w6", T.w6[:, :], [[16384, 2], [1, C]], 0, 0)
+    iota("clf", T.clf[:, :], [[16, 22]], 0, 0)
+    iota("lpf", T.lpf[:, :], [[1, 44]], 0, 0)
     for b in range(4):
         op("g", "one", "eb", g.affine_select, T.eb[:, 512 * b:512 * b + 512], T.one[:, :], [[-1, 512]], OP.is_equal, 0.0, b, 4)
     ts("par cf", "mk1", T.mk1[:, :], T.par[:, :], PH, 1e25, OP.is_equal, OP.mult)
@@ -236,21 +243,20 @@ def rank_program(g, core, T, topo):
     op("v", "ub", "uq", V.quantize_mx, T.uq[:, :], T.us[:, :], T.ub[:, :])
     cp("uq u6l", "u6", T.u6q[:, :].bitcast(dt.uint32), T.uq[:, :].bitcast(dt.uint32).indirect(T.u6l[:, 0:8]))
     act("uq u6l", "u6s", T.u6s[:, :], T.us[:, :].indirect(T.u6l[:, 0:8]))
-    need("s", ["xp0"], [])
-    dma("s", "d_w", "", "wq", T.wq[:, :].bitcast(dt.uint8), T.wc[:, :])
-    dma("s", "d_wp", "", "wp", T.wp[:, :], T.ws[:, :])
-    dma("s", "d_v", "", "vb", T.vb[:, :], T.v[:, :])
 
     def own_lists(r):
         sl, k = T["sl%d" % r], "sl%d" % r
-        ts(k, "tl", T.tl[:, 0:22], sl[:, 0:22], 528.0, None, OP.add)
-        ts(k, "tl", T.tl[:, 22:44], sl[:, 22:44], 176.0, None, OP.add)
+        ts(k, "sn", T.sn[:, :], sl[:, :], 176.0, None, OP.add)
+        ts(k, "tf", T.tf[:, 0:22], sl[:, 0:22], 528.0, None, OP.add)
+        ts(k, "tf", T.tf[:, 22:44], sl[:, 22:44], 176.0, None, OP.add)
         tten(k, "sd", T.sd[:, :], sl[:, 0:22], sl[:, 22:44], OP.subtract)
         ts(k, "fb", T.fb[:, 1:44:2], sl[:, 22:44], 176.0, None, OP.add)
         ts("sd", "fb", T.fb[:, 0:44:2], T.sd[:, :], 352.0, None, OP.add)
-        cp("fb", "fb", T.fb[:, 44:88], T.fb[:, 0:44])
-        cp("fb", "fb", T.fb[:, 88:176], T.fb[:, 0:88])
-        cp("fb", "fb", T.fb[:, 176:264], T.fb[:, 0:88])
+
+    def repeat_lists():
+        act("fb", "fb", T.fb[:, 44:88], T.fb[:, 0:44])
+        act("fb", "fb", T.fb[:, 88:176], T.fb[:, 0:88])
+        act("fb", "fb", T.fb[:, 176:264], T.fb[:, 0:88])
 
     def fetch(r):
         arrived("ld%d" % r, "la%d" % r, len(topo.engines(route(topo, partner(r), core)[0], core)))
@@ -263,50 +269,61 @@ def rank_program(g, core, T, topo):
 
     WF = " ".join("wf%d" % i for i in range(16))
 
-    def tables(r):
+    def choose():
         for e in range(2):
             ts("pl", "ll", T.ll[:, 44 * e:44 * e + 44], T.pl[:, :], 176.0 + 352.0 * e, None, OP.add)
+
+    def spread():
         act(WF + " lph", "pw", T.pw[:, :], T.wf[:, :].indirect(T.lph[:, :]))
-        for e in range(4):
-            o, a = T.s2[:, 512 * e:512 * e + C], T.pw[:, :].indirect(T.ll[:, 22 * e:22 * e + 22])
-            if r == 0 and e >= 2:
-                cp("pw ll", "s2", o, a)
-            else:
-                act("pw ll", "s2", o, a)
 
-    def bank(b, h):
-        return (T.pb if h else T.pa)[:, 512 * b:512 * b + 512], ("pb%d" if h else "pa%d") % b
+    def table(e, q):
+        o, a = T.s2[:, 512 * e:512 * e + C], T.pw[:, :].indirect(T.ll[:, 22 * e:22 * e + 22])
+        if q == "a":
+            act("pw ll", "s2%d" % e, o, a)
+        else:
+            cp("pw ll", "s2%d" % e, o, a)
 
-    def qx(r):
-        op("v", "xp%d pad%d" % (r, r), "xq", V.quantize_mx, T.xq[:, :], T.xs[:, :], T["xp%d" % r][:, :])
+    S2 = "s20 s21 s22 s23 s2g "
 
+    def bank(h, b):
+        n = HALF[h][1]
+        return ("pb%d" if h else "pa%d") % b, (T.pb if h else T.pa)[:, 512 * b:512 * b + n]
+
+    def plane(t, b):
+        return t[:, C * b:C * b + C]
+
+    def qx(r, h):
+        op("v", "xp%d0 xp%d1 pad%d" % (r, r, r), "xq%d" % h, V.quantize_mx, T.xq[:, 192 * h:192 * h + 192], T.xs[:, 192 * h:192 * h + 192],
+           T["xp%d" % r][:, 768 * h:768 * h + 768])
+
+    own_lists(0)
+    repeat_lists()
     for r in range(3):
         XP = T["xp%d" % r]
-        if r == 0:
-            own_lists(0)
-        qx(r)
-        mm("uq xq", "pb0", T.pb[:, 0:384], T.uq[:, :], T.us[:, :], T.xq[:, :], T.xs[:, :])
-        mm("u6 u6s xq", "pb1", T.pb[:, 512:512 + C], T.u6q[:, :], T.u6s[:, :], T.xq[:, 16:368], T.xs[:, 16:368])
-        act("xp%d" % r, "xh", T.xh[:, :], XP[:, 64:1472], scale=0.5)
-        act("pb1", "b6", T.b6[:, :], T.pb[:, 512:512 + C], AF.Sign, bias=-2.0 ** -93)
-        tten("pb0 mk1", "kk", T.kk[:, 0:352], T.pb[:, 16:368], T.mk1[:, 16:368], OP.is_gt)
-        tten("pb0 mk2", "kk", T.kk[:, 352:736], T.pb[:, 0:384], T.mk2[:, 0:384], OP.is_gt)
+        for h in range(2):
+            qx(r, h)
+            mm("uq xq%d" % h, "pb%d" % h, T.pb[:, 512 * h:512 * h + 192], T.uq[:, :], T.us[:, :], T.xq[:, 192 * h:192 * h + 192], T.xs[:, 192 * h:192 * h + 192])
+        mm("u6 u6s xq0 xq1", "pb2", T.pb[:, 1024:1024 + C], T.u6q[:, :], T.u6s[:, :], T.xq[:, 16:368], T.xs[:, 16:368])
+        for b in range(4):
+            act("xp%d0 xp%d1" % (r, r), "xh%d" % b, plane(T.xh, b), XP[:, 64 + b:1472:4], scale=0.5)
+        act("pb2", "b6", T.b6[:, :], T.pb[:, 1024:1024 + C], AF.Sign, bias=-2.0 ** -93)
+        for h in range(2):
+            tten("pb%d mk2" % h, "kk", T.kk[:, 352 + 192 * h:544 + 192 * h], T.pb[:, 512 * h:512 * h + 192], T.mk2[:, 192 * h:192 * h + 192], OP.is_gt)
+            a = 16 - 16 * h
+            tten("pb%d mk1" % h, "kk", T.kk[:, 176 * h:176 * h + 176], T.pb[:, 512 * h + a:512 * h + a + 176], T.mk1[:, 192 * h + a:192 * h + a + 176], OP.is_gt)
         op("v", "kk", "tt", V.transpose, T.tt[:, :], T.kk[:, :])
         for l in range(6):
-            a = 44 * l
-            tten("tt", "fm", T.fm[:, a + 1:a + 44:4], T.tt[:, l:352:32], T.tt[:, 368 + l:704:32], OP.add)
-            tten("tt", "fm", T.fm[:, a + 3:a + 44:4], T.tt[:, 384 + l:736:32], T.tt[:, 16 + l:352:32], OP.add)
+            tten("tt", "fm", T.fm[:, 44 * l + 1:44 * l + 44:2], T.tt[:, l:352:16], T.tt[:, 368 + l:720:16], OP.add)
         scan("fm fb", "fo", T.fo[:, :], T.fm[:, :], T.fb[:, :])
         cp("fo", "fl", T.fl[:, :], T.fo[:, 1:264:2])
         if r == 0:
             fetch(0)
-            ts("clf cf", "cl", T.cl[:, :], T.clf[:, :], PR, None, OP.add)
-            ts("cf", "cg", cg[:, 0:1], PR, 44.0, None, OP.mult)
-            ts("lpf cg", "lph", T.lph[:, :], T.lpf[:, :], cg[:, 0:1], None, OP.add)
-            ts("cf", "cg", cg[:, 1:2], P4, 704.0, None, OP.add)
-            ts("cf", "cg", cg[:, 2:3], P4, 352.0, 176.0, OP.mult, OP.add)
+            dma("s", "d_w", "", "wq", T.wq[:, :].bitcast(dt.uint8), T.wc[:, :])
+            dma("s", "d_wp", "", "wp", T.wp[:, :], T.ws[:, :])
+            dma("s", "d_v", "", "vb", T.vb[:, :], T.v[:, :])
         else:
-            tables(r)
+            choose()
+            spread()
         W, key = T.w6, "w6"
         for l in range(5, 0, -1):
             N_, nk = (T.wv0, "wv0") if l % 2 else (T.wv1, "wv1")
@@ -315,134 +332,130 @@ def rank_program(g, core, T, topo):
             cp(rk + " fl", nk + "a", N_[:, 0:352], W[:, :].indirect(off))
             act(rk + " fl", nk + "b", N_[:, 352:704], W[:, :].indirect(off), AF.Identity, bias=float(512 << (l - 1)))
             W, key = N_, nk
-            if r == 0:
-                if l == 5:
-                    ts("j16 cf", "m16", T.m16[:, 0:352], T.j16[:, 0:352], PR, None, OP.is_equal)
-                if l == 4:
-                    ts("j16", "r16", T.r16[:, 0:352], T.j16[:, 0:352], 0.0, None, OP.not_equal)
-                if l == 3:
-                    ts("j4 cf", "m4", T.m4[:, :], T.j4[:, :], PQ, None, OP.is_equal)
-                if l == 2:
-                    ts("j4", "r4", T.r4[:, :], T.j4[:, :], 0.0, None, OP.not_equal)
-        rk = key + "a " + key + "b fl"
-        win = W[:, :].indirect(T.fl[:, 0:22])
-        tten(rk + " m16", "wm", T.wm[:, :], win, T.m16[:, 0:352], OP.mult)
+            if r == 0 and l == 5:
+                ts("j16 cf", "m16", T.m16[:, 0:C], T.j16[:, :], PR, None, OP.is_equal)
+            if r == 0 and l == 4:
+                ts("clf cf", "cl", T.cl[:, :], T.clf[:, :], PR, None, OP.add)
+                ts("cf", "cg", cg[:, 0:1], PR, 44.0, None, OP.mult)
+                ts("lpf cg", "lph", T.lph[:, :], T.lpf[:, :], cg[:, 0:1], None, OP.add)
+        if r == 0:
+            choose()
+            spread()
+        for e in range(3):
+            table(e, "a")
+        tten(key + "a " + key + "b fl m16", "wm", T.wm[:, :], W[:, :].indirect(T.fl[:, 0:22]), T.m16[:, 0:352], OP.mult)
         scan("wm r16", "wsn", T.wsn[:, :], T.r16[:, 0:352], T.wm[:, :])
         cp("wsn", "vi", T.vi[:, :], T.wsn[:, 15:352:16])
-        ts("vi", "vk", T.vk[:, 0:22], T.vi[:, :], 0x600, None, OP.bitwise_and)
-        tten("vk cl", "ki", T.ki[:, :], T.vk[:, 0:22], T.cl[:, :], OP.add)
+        ts("vi", "vk0", T.vk[:, 0:22], T.vi[:, :], 0x600, None, OP.bitwise_and)
+        ts("vi", "vk3", T.vk[:, 66:88], T.vi[:, :], 511, None, OP.bitwise_and)
+        tten("vk0 cl", "ki", T.ki[:, :], T.vk[:, 0:22], T.cl[:, :], OP.add)
+        cp("vk3", "il", T.il[:, :], T.vk[:, 66:88])
         cp("ki", "k1", T.k1[:, :], T.ki[:, :])
-        ts("vi", "vk2", T.vk[:, 22:44], T.vi[:, :], 2, 0x600, OP.logical_shift_right, OP.bitwise_and)
-        ts("vi", "vk3", T.vk[:, 44:66], T.vi[:, :], 4, 0x600, OP.logical_shift_right, OP.bitwise_and)
-        tten(rk + " m4", "im", T.im[:, :], win, T.m4[:, :], OP.mult)
-        scan("im r4", "isn", T.isn[:, :], T.r4[:, :], T.im[:, :])
-        cp("isn", "ii", T.ii[:, :], T.isn[:, 3:352:4])
-        ts("ii", "ij", T.ij[:, :], T.ii[:, :], 511, None, OP.bitwise_and)
-        ts("ij cf", "ix", T.ix[:, :], T.ij[:, :], 4.0, P4, OP.mult, OP.add)
+        ts("vi", "vk1", T.vk[:, 22:44], T.vi[:, :], 2, 0x600, OP.logical_shift_right, OP.bitwise_and)
+        ts("vi", "vk2", T.vk[:, 44:66], T.vi[:, :], 4, 0x600, OP.logical_shift_right, OP.bitwise_and)
+        table(3, "v")
         if r == 0:
-            tables(0)
+            cp("m16", "m16", T.m16[:, 352:704], T.m16[:, 0:352])
+            op("v", "eb", "eq", V.quantize_mx, T.eq[:, :], T.es[:, :], T.eb[:, :])
         for h in range(2):
-            act("xh ix", "gi%d" % h, T.gi[:, 704 * h:704 * h + 704], T.xh[:, :].indirect(T.ix[:, 44 * h:44 * h + 44]))
-        for j in (1, 2):
-            tten("s2 k%d m16" % j, "km", T.km[:, :], T.s2[:, :].indirect(T["k%d" % j][:, :]), T.m16[:, 0:352], OP.mult)
-            scan("km r16", "ksn", T.ksn[:, :], T.r16[:, 0:352], T.km[:, :])
-            tten("ksn vk%d" % (j + 1), "ki", T.ki[:, :], T.ksn[:, 15:352:16], T.vk[:, 22 * j:22 * j + 22], OP.add)
-            ts("ki", "k%d" % (j + 1), T["k%d" % (j + 1)][:, :], T.ki[:, :], 176.0, None, OP.add)
-        tten("s2 k3 m4", "km", T.km[:, :], T.s2[:, :].indirect(T.k3[:, :]), T.m4[:, :], OP.mult)
-        scan("km r4", "ksn", T.ksn[:, :], T.r4[:, :], T.km[:, :])
-        ts("ksn cg", "kx", T.kx[:, :], T.ksn[:, 3:352:4], 4.0, cg[:, 1:2], OP.mult, OP.add)
-        def mosaic(h):
-            a = 704 * h
-            tten("xh kx gi%d" % h, "z%d" % h, T.z[:, a:a + 704], T.xh[:, :].indirect(T.kx[:, 44 * h:44 * h + 44]), T.gi[:, a:a + 704], OP.add)
-            op("v", "z%d" % h, "zq%d" % h, V.quantize_mx, T.zq[:, 176 * h:176 * h + 176], T.zs[:, 176 * h:176 * h + 176], T.z[:, a:a + 704])
+            a, n = HALF[h]
             for b in range(4):
-                o, k = bank(b, h)
-                mm("wq wp zq%d" % h, k, o[:, 0:176] if False else (T.pb if h else T.pa)[:, 512 * b:512 * b + 176], T.wq[:, 128 * b:128 * b + 128], T.wp[:, 128 * b:128 * b + 128], T.zq[:, 176 * h:176 * h + 176], T.zs[:, 176 * h:176 * h + 176])
+                act("xh%d il" % b, "gi%d%d" % (h, b), T.gi[:, 4 * a + b:4 * a + 4 * n:4], plane(T.xh, b).indirect(T.il[:, a // 16:(a + n) // 16]))
+        for j in (1, 2, 3):
+            tten(S2 + "k%d m16" % j, "km", T.km[:, :], T.s2[:, :].indirect(T["k%d" % j][:, :]), T.m16[:, 0:352], OP.mult)
+            scan("km r16", "ksn", T.ksn[:, :], T.r16[:, 0:352], T.km[:, :])
+            if j < 3:
+                tten("ksn vk%d" % j, "ki", T.ki[:, :], T.ksn[:, 15:352:16], T.vk[:, 22 * j:22 * j + 22], OP.add)
+                ts("ki", "k%d" % (j + 1), T["k%d" % (j + 1)][:, :], T.ki[:, :], 176.0, None, OP.add)
+            else:
+                ts("ksn", "k6", T.k6[:, :], T.ksn[:, 15:352:16], 176.0, None, OP.add)
+
+        def mosaic(h):
+            a, n = HALF[h]
+            for b in range(4):
+                v = slice(4 * a + b, 4 * a + 4 * n, 4)
+                tten("xh%d k6 gi%d%d" % (b, h, b), "z%d" % h, T.z[:, v], plane(T.xh, b).indirect(T.k6[:, a // 16:(a + n) // 16]), T.gi[:, v], OP.add)
+            op("v", "z%d" % h, "zq%d" % h, V.quantize_mx, T.zq[:, a:a + n], T.zs[:, a:a + n], T.z[:, 4 * a:4 * a + 4 * n])
+            for b in range(4):
+                k, o = bank(h, b)
+                mm("wq wp zq%d" % h, k, o, T.wq[:, 128 * b:128 * b + 128], T.wp[:, 128 * b:128 * b + 128], T.zq[:, a:a + n], T.zs[:, a:a + n])
 
         def hcast(h, b, q):
-            i = (T.pb if h else T.pa)[:, 512 * b:512 * b + 176]
-            o = T.hb[:, 704 * h + b:704 * h + 704:4]
-            k = ("pb%d" if h else "pa%d") % b
+            a, n = HALF[h]
+            k, i = bank(h, b)
+            o = T.hb[:, 4 * a + b:4 * a + 4 * n:4]
             if q == "a":
                 act(k, "hb%d%d" % (h, b), o, i, scale=0.03125)
             else:
                 ts(k, "hb%d%d" % (h, b), o, i, 0.03125, None, OP.mult)
 
         def qh(h):
-            op("v", " ".join("hb%d%d" % (h, b) for b in range(4)), "hq%d%d" % (r, h), V.quantize_mx, T["hq%d" % r][:, 176 * h:176 * h + 176],
-               T["hs%d" % r][:, 176 * h:176 * h + 176], T.hb[:, 704 * h:704 * h + 704])
+            a, n = HALF[h]
+            op("v", " ".join("hb%d%d" % (h, b) for b in range(4)), "hq%d%d" % (r, h), V.quantize_mx, T["hq%d" % r][:, a:a + n],
+               T["hs%d" % r][:, a:a + n], T.hb[:, 4 * a:4 * a + 4 * n])
             send_half(r, h)
 
         mosaic(0)
         for b in range(4):
             hcast(0, b, "a")
+        act("b6 k6", "en", T.en[:, :], T.b6[:, :].indirect(T.k6[:, :]))
         mosaic(1)
         qh(0)
-        tten("s2 k3 m16", "km", T.km[:, :], T.s2[:, :].indirect(T.k3[:, :]), T.m16[:, 0:352], OP.mult)
         hcast(1, 0, "a")
-        hcast(1, 2, "v")
-        hcast(1, 1, "a")
+        hcast(1, 1, "v")
+        hcast(1, 2, "a")
         hcast(1, 3, "v")
         qh(1)
-        scan("km r16", "ksn", T.ksn[:, :], T.r16[:, 0:352], T.km[:, :])
-        ts("ksn", "k6", T.k6[:, :], T.ksn[:, 15:352:16], 176.0, None, OP.add)
-        act("b6 k6", "en", T.en[:, :], T.b6[:, :].indirect(T.k6[:, :]))
-        if r == 0:
-            ts("j16 cf", "m16", T.m16[:, 352:704], T.j16[:, 352:704], PR, None, OP.is_equal)
-            ts("j16", "r16", T.r16[:, 352:704], T.j16[:, 352:704], 0.0, None, OP.not_equal)
-        tten("pw", "dp", T.dp[:, :], T.pw[:, 1:704:2], T.pw[:, 0:704:2], OP.subtract)
-        tten("en", "dd", T.dd[:, :], T.en[:, 0:352:2], T.en[:, 1:352:2], OP.not_equal)
-        for b in range(2):
-            tten("dd dp", "xx", T.xx[:, 176 * b:176 * b + 176], T.dp[:, 176 * b:176 * b + 176], T.dd[:, :], OP.mult)
-        tten("pw xx", "pt", T.pt[:, 0:704:2], T.pw[:, 0:704:2], T.xx[:, :], OP.add)
-        tten("pw xx", "pt", T.pt[:, 1:704:2], T.pw[:, 1:704:2], T.xx[:, :], OP.subtract)
+        tten("en", "dd", T.dd[:, 0:352:2], T.en[:, 0:352:2], T.en[:, 1:352:2], OP.not_equal)
+        ts("dd", "dd", T.dd[:, 1:352:2], T.dd[:, 0:352:2], -1.0, None, OP.mult)
+        tten("dd sn m16", "tm", T.tm[:, :], T.dd[:, :].indirect(T.sn[:, :]), T.m16[:, :], OP.mult)
+        scan("tm r16", "ts", T.ts[:, :], T.r16[:, :], T.tm[:, :])
+        tten("ts tf", "tg", T.tg[:, :], T.ts[:, 15:704:16], T.tf[:, :], OP.add)
+        cp("tg", "tl", T.tl[:, :], T.tg[:, :])
+        lo = 0 if r < 2 else 352
+        tten("pw tl m16", "tm", T.tm[:, lo:704], T.pw[:, :].indirect(T.tl[:, lo // 16:44]), T.m16[:, lo:704], OP.mult)
+        scan("tm r16", "ts", T.ts[:, lo:704], T.r16[:, lo:704], T.tm[:, lo:704])
         if r < 2:
-            tten("pt tl m16", "tm", T.tm[:, :], T.pt[:, :].indirect(T.tl[:, :]), T.m16[:, :], OP.mult)
-            scan("tm r16", "ts", T.ts[:, :], T.r16[:, :], T.tm[:, :])
             cp("ts", "sl%d" % (r + 1), T["sl%d" % (r + 1)][:, :], T.ts[:, 15:704:16])
             send_list(r + 1)
             fetch(r + 1)
-        tten("pt tl m4", "t4", T.t4[:, :], T.pt[:, :].indirect(T.tl[:, 22:44]), T.m4[:, :], OP.mult)
-        scan("t4 r4", "t4s", T.t4s[:, :], T.r4[:, :], T.t4[:, :])
-        ts("t4s cg", "tx", T.tx[:, :], T.t4s[:, 3:352:4], cg[:, 2:3], None, OP.add)
+        ts("ts", "tx", T.tx[:, :], T.ts[:, 367:704:16], 176.0, None, OP.add)
         if r < 2:
             own_lists(r + 1)
-        if r == 0:
-            op("v", "eb", "eq", V.quantize_mx, T.eq[:, :], T.es[:, :], T.eb[:, :])
+        else:
             op("v", "vb", "vq", V.quantize_mx, T.vq[:, :], T.vs[:, :], T.vb[:, :])
         hp = route(topo, partner(r), core)
         for h in range(2):
+            a, n = HALF[h]
             arrived("dq%d%d" % (r, h), ("ca%d" if h == 0 else "cb%d") % r, sum(2 * len(topo.engines(k, core)) for k in hp[2 * h:2 * h + 2]))
             for b in range(4):
-                ps = (T.pb if h else T.pa)[:, 512 * b:512 * b + 176]
-                k = ("pb%d" if h else "pa%d") % b
+                k, ps = bank(h, b)
                 mm("eq dq%d%d" % (r, h), k, ps, T.eq[:, 128 * b:128 * b + 128], T.es[:, 128 * b:128 * b + 128],
-                   T["dq%d" % r][:, 176 * h:176 * h + 176], T["ds%d" % r][:, 176 * h:176 * h + 176])
+                   T["dq%d" % r][:, a:a + n], T["ds%d" % r][:, a:a + n])
             for b in range(4):
-                ps = (T.pb if h else T.pa)[:, 512 * b:512 * b + 176]
-                k = ("pb%d" if h else "pa%d") % b
-                o = T.dw[:, 352 * b + 176 * h:352 * b + 176 * h + 176]
-                if h == 0 or b < 2:
+                k, ps = bank(h, b)
+                o = T.dw[:, C * b + a:C * b + a + n]
+                if h == 0 or b % 2 == 0:
                     act(k, "dw%d%d" % (h, b), o, ps)
                 else:
                     cp(k, "dw%d%d" % (h, b), o, ps)
-        tten("tx xp%d " % r + " ".join("dw%d%d" % (h, b) for h in range(2) for b in range(4)), "xp%d" % (r + 1),
-             T["xp%d" % (r + 1)][:, 64:1472], T.dw[:, :].indirect(T.tx[:, :]), XP[:, 64:1472], OP.add)
+        if r < 2:
+            repeat_lists()
+        for b in range(4):
+            v = slice(64 + b, 1472, 4)
+            tten("tx xp%d0 xp%d1 dw0%d dw1%d" % (r, r, b, b), "xp%d0" % (r + 1), T["xp%d" % (r + 1)][:, v], plane(T.dw, b).indirect(T.tx[:, :]), XP[:, v], OP.add)
 
-    act("pt tl", "tw", T.tw[:, :], T.pt[:, :].indirect(T.tl[:, :]), AF.Identity, bias=176.0)
+    act("pw tl", "tw", T.tw[:, :], T.pw[:, :].indirect(T.tl[:, :]), AF.Identity, bias=176.0)
     dma("s", "d_so", "tw", "so", T.so[:, 0:352], T.tw[0:128:16, 352:704])
     dma("s", "d_so", "tw", "so2", T.so[:, 352:704], T.tw[0:128:16, 0:352])
-    qx(3)
-    dma("s", "d_oc", "xq", "oc", T.oc[:, :], T.xq[:, 16:368].bitcast(dt.uint8))
+    qx(3, 0)
+    qx(3, 1)
+    dma("s", "d_oc", "xq0 xq1", "oc", T.oc[:, :], T.xq[:, 16:368].bitcast(dt.uint8))
     for k in range(4):
-        dma("s", "d_oc", "xq", "osc%d" % k, T.osc[4 * k:4 * k + 4, :], T.xs[32 * k:32 * k + 4, 16:368])
-    mm("vq xq", "pa0", T.pa[:, 0:C], T.vq[:, :], T.vs[:, :], T.xq[:, 16:368], T.xs[:, 16:368])
+        dma("s", "d_oc", "xq0 xq1", "osc%d" % k, T.osc[4 * k:4 * k + 4, :], T.xs[32 * k:32 * k + 4, 16:368])
+    mm("vq xq0 xq1", "pa0", T.pa[:, 0:C], T.vq[:, :], T.vs[:, :], T.xq[:, 16:368], T.xs[:, 16:368])
     cp("pa0", "yb", T.yb[:, :], T.pa[:, 0:C])
-    dma("s", "d_y", "yb", "y", T.y[:, :], T.yb[:, :])
+    dma("a", "d_y", "yb", "y", T.y[:, :], T.yb[:, :])
     total["ls"] = sent[0]
     for s in total:
         g.wait_ge(T.sem[s], total[s])
-
-
-SCRATCH["wv0"] = ("sbuf", [128, 704], F32)
-SCRATCH["wv1"] = ("sbuf", [128, 704], F32)

from concourse.bass import DstId, RemoteDMATransfer
from concourse.mybir import dt, AluOpType as OP, ActivationFunctionType as AF

C = 352
MASK = [2, 4, 1]
HALF = [(0, 192), (192, 160)]
BF, F32, I32, U16, U8, E4 = "bfloat16", "float32", "int32", "uint16", "uint8", "float8_e4m3fn_x4"
SCRATCH = {
    "sei": ("sbuf", [128, 44], I32), "ub": ("sbuf", [128, 512], BF), "vb": ("sbuf", [128, 512], BF),
    "wq": ("sbuf", [128, 512], E4), "wp": ("sbuf", [128, 512], U8),
    "uq": ("sbuf", [128, 128], E4), "us": ("sbuf", [128, 128], U8), "vq": ("sbuf", [128, 128], E4), "vs": ("sbuf", [128, 128], U8),
    "u6q": ("sbuf", [128, 128], E4), "u6s": ("sbuf", [128, 128], U8),
    "pc": ("sbuf", [128, 8], I32), "ci": ("sbuf", [128, 8], I32), "cf": ("sbuf", [128, 8], F32), "cg": ("sbuf", [128, 8], F32),
    "par": ("sbuf", [128, 384], F32), "mk1": ("sbuf", [128, 384], F32), "mk2": ("sbuf", [128, 384], F32),
    "j16": ("sbuf", [128, C], F32), "w6": ("sbuf", [128, 704], F32), "m16": ("sbuf", [128, 704], BF), "r16": ("sbuf", [128, 704], BF),
    "clf": ("sbuf", [128, 22], F32), "cl": ("sbuf", [128, 22], I32), "lpf": ("sbuf", [128, 44], F32), "lph": ("sbuf", [128, 44], U16),
    "u6f": ("sbuf", [128, 8], F32), "u6l": ("sbuf", [128, 8], U16),
    "one": ("sbuf", [128, 512], BF), "eb": ("sbuf", [128, 2048], BF), "eq": ("sbuf", [128, 512], E4), "es": ("sbuf", [128, 512], U8),
    "xq": ("sbuf", [128, 384], E4), "xs": ("sbuf", [128, 384], U8), "xh": ("sbuf", [128, 1408], BF), "b6": ("sbuf", [128, C], BF),
    "kk": ("sbuf", [128, 736], BF), "tt": ("sbuf", [128, 736], BF), "fm": ("sbuf", [128, 264], F32), "fb": ("sbuf", [128, 264], F32),
    "fo": ("sbuf", [128, 264], F32), "fl": ("sbuf", [128, 132], U16), "sd": ("sbuf", [128, 22], F32),
    "wv0": ("sbuf", [128, 704], F32), "wv1": ("sbuf", [128, 704], F32),
    "wm": ("sbuf", [128, C], F32), "wsn": ("sbuf", [128, C], F32), "vi": ("sbuf", [128, 22], I32), "vk": ("sbuf", [128, 88], I32),
    "il": ("sbuf", [128, 22], U16),
    "wf": ("sbuf", [128, 704], BF), "pl": ("sbuf", [128, 44], BF), "ll": ("sbuf", [128, 88], U16), "pw": ("sbuf", [128, 704], BF),
    "s2": ("sbuf", [128, 2048], BF), "km": ("sbuf", [128, C], BF), "ksn": ("sbuf", [128, C], BF),
    "ki": ("sbuf", [128, 22], I32), "k1": ("sbuf", [128, 22], U16), "k2": ("sbuf", [128, 22], U16), "k3": ("sbuf", [128, 22], U16),
    "k6": ("sbuf", [128, 22], U16),
    "sn": ("sbuf", [128, 44], U16), "tf": ("sbuf", [128, 44], F32), "tg": ("sbuf", [128, 44], F32), "tl": ("sbuf", [128, 44], U16),
    "en": ("sbuf", [128, C], BF), "dd": ("sbuf", [128, C], BF), "tm": ("sbuf", [128, 704], BF), "ts": ("sbuf", [128, 704], BF),
    "tx": ("sbuf", [128, 22], U16), "tw": ("sbuf", [128, 704], F32),
    "gi": ("sbuf", [128, 1408], BF), "z": ("sbuf", [128, 1408], BF), "zq": ("sbuf", [128, C], E4), "zs": ("sbuf", [128, C], U8),
    "hb": ("sbuf", [128, 1408], BF), "dw": ("sbuf", [128, 1408], BF), "yb": ("sbuf", [128, C], F32),
    "pa": ("psum", [128, 2048], F32), "pb": ("psum", [128, 2048], F32),
}
for _r in range(4):
    SCRATCH["xp%d" % _r] = ("sbuf", [128, 1536], BF)
for _r in range(3):
    SCRATCH["sl%d" % _r] = ("sbuf", [128, 44], BF)
    SCRATCH["lh%d" % _r] = ("sbuf", [128, 44], BF)
    SCRATCH["ld%d" % _r] = ("dram", [128, 44], BF)
    SCRATCH["hq%d" % _r] = ("sbuf", [128, C], E4)
    SCRATCH["hs%d" % _r] = ("sbuf", [128, C], U8)
    SCRATCH["fq%d" % _r] = ("sbuf", [128, 96], E4)
    SCRATCH["fs%d" % _r] = ("sbuf", [128, 96], U8)
    SCRATCH["dq%d" % _r] = ("sbuf", [128, C], E4)
    SCRATCH["ds%d" % _r] = ("sbuf", [128, C], U8)
SEMAPHORES = ["sv", "sa", "sp", "sg", "ls"] + ["d_" + n for n in ("se", "x", "x2", "u", "w", "wp", "v", "y", "oc", "so")]
for _r in range(3):
    SEMAPHORES += [n + str(_r) for n in ("hl", "hc", "hp", "la", "ca", "cb", "rp")]


def route(topo, core, dst):
    ok = [h for h in topo.cores_of(core) if h != core and topo.may_write(h, dst)]
    near = [h for h in ok if topo.die(h) == topo.die(core)]
    far = [h for h in ok if topo.die(h) != topo.die(core)]
    return [near[0], far[0], near[1], far[1]]


def chunk(i):
    a, n = HALF[i // 2]
    return a + n // 2 * (i % 2), n // 2


def bits(e):
    return sum(1 << i for i in e)


def hand_on(g, core, T, topo):
    mine = [c for c in T.cores if c in topo.cores_of(core)]
    sent = 0
    for r in range(3):
        for c in mine:
            dst = T.cores[T.rank_of(c) ^ MASK[r]]
            hs = route(topo, c, dst)
            if core not in hs:
                continue
            i = hs.index(core)
            rid, pid = topo.addr(dst, core)
            e = topo.engines(core, dst)
            n_in = len(topo.engines(c, core)) // 2
            if i == 0:
                g.wait_ge(T.sem["hl%d" % r], n_in)
                g.remote_dma(T["ld%d" % r][:, :], T["lh%d" % r][:, :], T.sem["la%d" % r], T.sem.ls, pid, rid, bits(e))
                sent += len(e)
            arr = T.sem[("ca%d" if i < 2 else "cb%d") % r]
            a, n = chunk(i)
            g.wait_ge(T.sem["hc%d" % r], n_in)
            g.remote_dma(T["dq%d" % r][:, a:a + n].bitcast(dt.uint8), T["fq%d" % r][:, 0:n].bitcast(dt.uint8), arr, T.sem.ls, pid, rid, bits(e))
            g.wait_ge(T.sem["hp%d" % r], n_in)
            g.remote_dma(T["ds%d" % r][:, a:a + n], T["fs%d" % r][:, 0:n], arr, T.sem.ls, pid, rid, bits(e))
            sent += 2 * len(e)
    if sent:
        g.wait_ge(T.sem.ls, sent)


def rank_program(g, core, T, topo):
    rank = T.rank_of(core)
    if rank is None:
        hand_on(g, core, T, topo)
        return
    eng = {"v": g.vector, "a": g.scalar, "p": g.tensor, "g": g, "s": g.sync}
    sem_of = {"v": "sv", "a": "sa", "p": "sp", "g": "sg"}
    total, seen = {}, {}
    last, readers = {}, {}

    def need(q, r, w):
        d = {}
        for k in r:
            t = last.get(k)
            if t is not None:
                d[t[0]] = max(d.get(t[0], 0), t[1])
        for k in w:
            for t in readers.get(k, []) + ([last[k]] if k in last else []):
                if t[2] != q or t[0][0:2] == "d_":
                    d[t[0]] = max(d.get(t[0], 0), t[1])
        for s in d:
            if seen.get((q, s), 0) < d[s]:
                eng[q].wait_ge(T.sem[s], d[s])
                seen[(q, s)] = d[s]

    def mark(t, r, w):
        for k in r:
            readers[k] = [x for x in readers.get(k, []) if x[0] != t[0]] + [t]
        for k in w:
            last[k] = t
            readers[k] = []

    def op(q, r, w, f, *args, **kw):
        r, w = r.split(), w.split()
        need(q, r, w)
        s = sem_of[q]
        f(*args, **kw).then_inc(T.sem[s], 1)
        total[s] = total.get(s, 0) + 1
        mark((s, total[s], q), r, w)

    def dma(q, sem, r, w, out, in_):
        r, w = r.split(), w.split()
        need(q, r, w)
        eng[q].dma_start(out, in_).then_inc(T.sem[sem], 16)
        total[sem] = total.get(sem, 0) + 16
        mark((sem, total[sem], q), r, w)

    V, A, P = g.vector, g.scalar, g.tensor

    def ts(r, w, out, in0, s1, s2, o0, o1=None):
        if o1 is None:
            op("v", r, w, V.tensor_scalar, out, in0, s1, s2, o0)
        else:
            op("v", r, w, V.tensor_scalar, out, in0, s1, s2, o0, o1)

    def tten(r, w, out, a, b, o):
        op("v", r, w, V.tensor_tensor, out, a, b, o)

    def cp(r, w, out, in_):
        op("v", r, w, V.tensor_copy, out, in_)

    def scan(r, w, out, d0, d1):
        op("v", r, w, V.tensor_tensor_scan, out, d0, d1, 0.0, OP.mult, OP.add)

    def act(r, w, out, in_, func=AF.Copy, **kw):
        op("a", r, w, A.activation, out, in_, func, **kw)

    def mm(r, w, out, wq, wsc, xq, xsc):
        op("p", r, w, P.matmul_mx, out, wq, wsc, xq, xsc, True, True)

    def arrived(key, sem, n):
        total[sem] = n
        last[key] = (sem, n, "r")
        readers[key] = []

    dma("s", "d_se", "", "sei", T.sei[:, :], T.se[:, :])
    dma("s", "d_x", "", "xp00", T.xp0[:, 64:768], T.x[:, 0:704])
    dma("a", "d_u", "", "ub", T.ub[:, :], T.u[:, :])
    dma("a", "d_x2", "", "xp01", T.xp0[:, 768:1472], T.x[:, 704:1408])

    def iota(k, out, pattern, base, cm):
        op("g", "", k, g.iota, out, pattern, base, cm, allow_small_or_imprecise_dtypes=True)

    op("g", "", "pc", g.iota, T.pc[:, 0:1], [[0, 1]], 0, 1)
    iota("u6f", T.u6f[:, :], [[16, 8]], 6, 0)
    iota("par", T.par[:, :], [[0, 12], [1, 2], [0, 16]], 0, 0)
    iota("j16", T.j16[:, :], [[0, 22], [1, 16]], 0, 0)
    for r in range(4):
        op("v", "", "pad%d" % r, V.memset, T["xp%d" % r][:, 0:64], 0.0)
        op("v", "", "pad%d" % r, V.memset, T["xp%d" % r][:, 1472:1536], 0.0)
    op("v", "", "one", V.memset, T.one[:, :], 1.0)
    for e in range(4):
        op("v", "", "s2g", V.memset, T.s2[:, 512 * e + C:512 * e + 512], 0.0)
    op("v", "", "r16o", V.memset, T.r16[:, :], 1.0)
    op("v", "r16o", "r16", V.memset, T.r16[:, 0:704:16], 0.0)
    op("v", "", "fm", V.memset, T.fm[:, :], 0.0)
    ci, cf, cg = T.ci, T.cf, T.cg
    ts("pc", "ci", ci[:, 0:1], T.pc[:, 0:1], 15, None, OP.bitwise_and)
    ts("pc", "ci", ci[:, 1:2], T.pc[:, 0:1], 4, 1, OP.logical_shift_right, OP.bitwise_and)
    cp("u6f", "u6l", T.u6l[:, :], T.u6f[:, :])
    cp("ci", "cf", cf[:, 0:2], ci[:, 0:2])
    PR, PH = cf[:, 0:1], cf[:, 1:2]
    ts("sei", "sl0", T.sl0[:, 0:22], T.sei[:, 22:44], -176.0, None, OP.add)
    ts("sei", "sl0", T.sl0[:, 22:44], T.sei[:, 0:22], -176.0, None, OP.add)

    sent = [0]

    def partner(r):
        return T.cores[rank ^ MASK[r]]

    def send_list(r):
        h = route(topo, core, partner(r))[0]
        rid, pid = topo.addr(h, core)
        e = topo.engines(core, h)
        e = e[:len(e) // 2]
        need("g", ["sl%d" % r], [])
        g.remote_dma(T["lh%d" % r][:, :], T["sl%d" % r][:, :], T.sem["hl%d" % r], T.sem.ls, pid, rid, bits(e))
        sent[0] += len(e)

    def send_half(r, h):
        hs = route(topo, core, partner(r))[2 * h:2 * h + 2]
        for codes in (True, False):
            tr = []
            for i, k in enumerate(hs):
                rid, pid = topo.addr(k, core)
                e = topo.engines(core, k)
                n = len(e) // 2
                a, m = chunk(2 * h + i)
                if codes:
                    s, d = T["hq%d" % r][:, a:a + m].bitcast(dt.uint8), T["fq%d" % r][:, 0:m].bitcast(dt.uint8)
                else:
                    s, d = T["hs%d" % r][:, a:a + m], T["fs%d" % r][:, 0:m]
                tr.append(RemoteDMATransfer(dst_ids=[DstId(rid=rid, pnc=pid)], dma_engine_mask=bits(e[n * i:n * i + n]),
                                            remote_sem=T.sem[("hc%d" if codes else "hp%d") % r], src=s, dst=d))
                sent[0] += n
            need("g", ["hq%d%d" % (r, h)], [])
            g.remote_dma_fused(tr, local_sem=T.sem.ls)

    send_list(0)
    iota("w6", T.w6[:, :], [[16384, 2], [1, C]], 0, 0)
    iota("clf", T.clf[:, :], [[16, 22]], 0, 0)
    iota("lpf", T.lpf[:, :], [[1, 44]], 0, 0)
    for b in range(4):
        op("g", "one", "eb", g.affine_select, T.eb[:, 512 * b:512 * b + 512], T.one[:, :], [[-1, 512]], OP.is_equal, 0.0, b, 4)
    ts("par cf", "mk1", T.mk1[:, :], T.par[:, :], PH, 1e25, OP.is_equal, OP.mult)
    ts("par cf", "mk2", T.mk2[:, :], T.par[:, :], PH, 1e25, OP.not_equal, OP.mult)
    op("v", "ub", "uq", V.quantize_mx, T.uq[:, :], T.us[:, :], T.ub[:, :])
    cp("uq u6l", "u6", T.u6q[:, :].bitcast(dt.uint32), T.uq[:, :].bitcast(dt.uint32).indirect(T.u6l[:, 0:8]))
    act("uq u6l", "u6s", T.u6s[:, :], T.us[:, :].indirect(T.u6l[:, 0:8]))

    def own_lists(r):
        sl, k = T["sl%d" % r], "sl%d" % r
        ts(k, "sn", T.sn[:, :], sl[:, :], 176.0, None, OP.add)
        ts(k, "tf", T.tf[:, 0:22], sl[:, 0:22], 528.0, None, OP.add)
        ts(k, "tf", T.tf[:, 22:44], sl[:, 22:44], 176.0, None, OP.add)
        tten(k, "sd", T.sd[:, :], sl[:, 0:22], sl[:, 22:44], OP.subtract)
        ts(k, "fb", T.fb[:, 1:44:2], sl[:, 22:44], 176.0, None, OP.add)
        ts("sd", "fb", T.fb[:, 0:44:2], T.sd[:, :], 352.0, None, OP.add)

    def repeat_lists():
        act("fb", "fb", T.fb[:, 44:88], T.fb[:, 0:44])
        act("fb", "fb", T.fb[:, 88:176], T.fb[:, 0:88])
        act("fb", "fb", T.fb[:, 176:264], T.fb[:, 0:88])

    def fetch(r):
        arrived("ld%d" % r, "la%d" % r, len(topo.engines(route(topo, partner(r), core)[0], core)))
        ld = T["ld%d" % r]
        dma("s", "rp%d" % r, "ld%d" % r, "pl", T.pl[:, :], ld[:, :])
        for i in range(16):
            dma("s", "rp%d" % r, "ld%d" % r, "wf%d" % i, T.wf[i:128:16, :], ld[:, :])
        for k in ["pl"] + ["wf%d" % i for i in range(16)]:
            last[k] = ("rp%d" % r, total["rp%d" % r], "s")

    WF = " ".join("wf%d" % i for i in range(16))

    def choose():
        for e in range(2):
            ts("pl", "ll", T.ll[:, 44 * e:44 * e + 44], T.pl[:, :], 176.0 + 352.0 * e, None, OP.add)

    def spread():
        act(WF + " lph", "pw", T.pw[:, :], T.wf[:, :].indirect(T.lph[:, :]))

    def table(e, q):
        o, a = T.s2[:, 512 * e:512 * e + C], T.pw[:, :].indirect(T.ll[:, 22 * e:22 * e + 22])
        if q == "a":
            act("pw ll", "s2%d" % e, o, a)
        else:
            cp("pw ll", "s2%d" % e, o, a)

    S2 = "s20 s21 s22 s23 s2g "

    def bank(h, b):
        n = HALF[h][1]
        return ("pb%d" if h else "pa%d") % b, (T.pb if h else T.pa)[:, 512 * b:512 * b + n]

    def plane(t, b):
        return t[:, C * b:C * b + C]

    def qx(r, h):
        op("v", "xp%d0 xp%d1 pad%d" % (r, r, r), "xq%d" % h, V.quantize_mx, T.xq[:, 192 * h:192 * h + 192], T.xs[:, 192 * h:192 * h + 192],
           T["xp%d" % r][:, 768 * h:768 * h + 768])

    own_lists(0)
    repeat_lists()
    for r in range(3):
        XP = T["xp%d" % r]
        for h in range(2):
            qx(r, h)
            mm("uq xq%d" % h, "pb%d" % h, T.pb[:, 512 * h:512 * h + 192], T.uq[:, :], T.us[:, :], T.xq[:, 192 * h:192 * h + 192], T.xs[:, 192 * h:192 * h + 192])
        mm("u6 u6s xq0 xq1", "pb2", T.pb[:, 1024:1024 + C], T.u6q[:, :], T.u6s[:, :], T.xq[:, 16:368], T.xs[:, 16:368])
        for b in range(4):
            act("xp%d0 xp%d1" % (r, r), "xh%d" % b, plane(T.xh, b), XP[:, 64 + b:1472:4], scale=0.5)
        act("pb2", "b6", T.b6[:, :], T.pb[:, 1024:1024 + C], AF.Sign, bias=-2.0 ** -93)
        for h in range(2):
            tten("pb%d mk2" % h, "kk", T.kk[:, 352 + 192 * h:544 + 192 * h], T.pb[:, 512 * h:512 * h + 192], T.mk2[:, 192 * h:192 * h + 192], OP.is_gt)
            a = 16 - 16 * h
            tten("pb%d mk1" % h, "kk", T.kk[:, 176 * h:176 * h + 176], T.pb[:, 512 * h + a:512 * h + a + 176], T.mk1[:, 192 * h + a:192 * h + a + 176], OP.is_gt)
        op("v", "kk", "tt", V.transpose, T.tt[:, :], T.kk[:, :])
        for l in range(6):
            tten("tt", "fm", T.fm[:, 44 * l + 1:44 * l + 44:2], T.tt[:, l:352:16], T.tt[:, 368 + l:720:16], OP.add)
        scan("fm fb", "fo", T.fo[:, :], T.fm[:, :], T.fb[:, :])
        cp("fo", "fl", T.fl[:, :], T.fo[:, 1:264:2])
        if r == 0:
            fetch(0)
            dma("s", "d_w", "", "wq", T.wq[:, :].bitcast(dt.uint8), T.wc[:, :])
            dma("s", "d_wp", "", "wp", T.wp[:, :], T.ws[:, :])
            dma("s", "d_v", "", "vb", T.vb[:, :], T.v[:, :])
        else:
            choose()
            spread()
        W, key = T.w6, "w6"
        for l in range(5, 0, -1):
            N_, nk = (T.wv0, "wv0") if l % 2 else (T.wv1, "wv1")
            off = T.fl[:, 22 * l:22 * l + 22]
            rk = key if key == "w6" else key + "a " + key + "b"
            cp(rk + " fl", nk + "a", N_[:, 0:352], W[:, :].indirect(off))
            act(rk + " fl", nk + "b", N_[:, 352:704], W[:, :].indirect(off), AF.Identity, bias=float(512 << (l - 1)))
            W, key = N_, nk
            if r == 0 and l == 5:
                ts("j16 cf", "m16", T.m16[:, 0:C], T.j16[:, :], PR, None, OP.is_equal)
            if r == 0 and l == 4:
                ts("clf cf", "cl", T.cl[:, :], T.clf[:, :], PR, None, OP.add)
                ts("cf", "cg", cg[:, 0:1], PR, 44.0, None, OP.mult)
                ts("lpf cg", "lph", T.lph[:, :], T.lpf[:, :], cg[:, 0:1], None, OP.add)
        if r == 0:
            choose()
            spread()
        for e in range(3):
            table(e, "a")
        tten(key + "a " + key + "b fl m16", "wm", T.wm[:, :], W[:, :].indirect(T.fl[:, 0:22]), T.m16[:, 0:352], OP.mult)
        scan("wm r16", "wsn", T.wsn[:, :], T.r16[:, 0:352], T.wm[:, :])
        cp("wsn", "vi", T.vi[:, :], T.wsn[:, 15:352:16])
        ts("vi", "vk0", T.vk[:, 0:22], T.vi[:, :], 0x600, None, OP.bitwise_and)
        ts("vi", "vk3", T.vk[:, 66:88], T.vi[:, :], 511, None, OP.bitwise_and)
        tten("vk0 cl", "ki", T.ki[:, :], T.vk[:, 0:22], T.cl[:, :], OP.add)
        cp("vk3", "il", T.il[:, :], T.vk[:, 66:88])
        cp("ki", "k1", T.k1[:, :], T.ki[:, :])
        ts("vi", "vk1", T.vk[:, 22:44], T.vi[:, :], 2, 0x600, OP.logical_shift_right, OP.bitwise_and)
        ts("vi", "vk2", T.vk[:, 44:66], T.vi[:, :], 4, 0x600, OP.logical_shift_right, OP.bitwise_and)
        table(3, "v")
        if r == 0:
            cp("m16", "m16", T.m16[:, 352:704], T.m16[:, 0:352])
            op("v", "eb", "eq", V.quantize_mx, T.eq[:, :], T.es[:, :], T.eb[:, :])
        for h in range(2):
            a, n = HALF[h]
            for b in range(4):
                act("xh%d il" % b, "gi%d%d" % (h, b), T.gi[:, 4 * a + b:4 * a + 4 * n:4], plane(T.xh, b).indirect(T.il[:, a // 16:(a + n) // 16]))
        for j in (1, 2, 3):
            tten(S2 + "k%d m16" % j, "km", T.km[:, :], T.s2[:, :].indirect(T["k%d" % j][:, :]), T.m16[:, 0:352], OP.mult)
            scan("km r16", "ksn", T.ksn[:, :], T.r16[:, 0:352], T.km[:, :])
            if j < 3:
                tten("ksn vk%d" % j, "ki", T.ki[:, :], T.ksn[:, 15:352:16], T.vk[:, 22 * j:22 * j + 22], OP.add)
                ts("ki", "k%d" % (j + 1), T["k%d" % (j + 1)][:, :], T.ki[:, :], 176.0, None, OP.add)
            else:
                ts("ksn", "k6", T.k6[:, :], T.ksn[:, 15:352:16], 176.0, None, OP.add)

        def mosaic(h):
            a, n = HALF[h]
            for b in range(4):
                v = slice(4 * a + b, 4 * a + 4 * n, 4)
                tten("xh%d k6 gi%d%d" % (b, h, b), "z%d" % h, T.z[:, v], plane(T.xh, b).indirect(T.k6[:, a // 16:(a + n) // 16]), T.gi[:, v], OP.add)
            op("v", "z%d" % h, "zq%d" % h, V.quantize_mx, T.zq[:, a:a + n], T.zs[:, a:a + n], T.z[:, 4 * a:4 * a + 4 * n])
            for b in range(4):
                k, o = bank(h, b)
                mm("wq wp zq%d" % h, k, o, T.wq[:, 128 * b:128 * b + 128], T.wp[:, 128 * b:128 * b + 128], T.zq[:, a:a + n], T.zs[:, a:a + n])

        def hcast(h, b, q):
            a, n = HALF[h]
            k, i = bank(h, b)
            o = T.hb[:, 4 * a + b:4 * a + 4 * n:4]
            if q == "a":
                act(k, "hb%d%d" % (h, b), o, i, scale=0.03125)
            else:
                ts(k, "hb%d%d" % (h, b), o, i, 0.03125, None, OP.mult)

        def qh(h):
            a, n = HALF[h]
            op("v", " ".join("hb%d%d" % (h, b) for b in range(4)), "hq%d%d" % (r, h), V.quantize_mx, T["hq%d" % r][:, a:a + n],
               T["hs%d" % r][:, a:a + n], T.hb[:, 4 * a:4 * a + 4 * n])
            send_half(r, h)

        mosaic(0)
        for b in range(4):
            hcast(0, b, "a")
        act("b6 k6", "en", T.en[:, :], T.b6[:, :].indirect(T.k6[:, :]))
        mosaic(1)
        qh(0)
        hcast(1, 0, "a")
        hcast(1, 1, "v")
        hcast(1, 2, "a")
        hcast(1, 3, "v")
        qh(1)
        tten("en", "dd", T.dd[:, 0:352:2], T.en[:, 0:352:2], T.en[:, 1:352:2], OP.not_equal)
        ts("dd", "dd", T.dd[:, 1:352:2], T.dd[:, 0:352:2], -1.0, None, OP.mult)
        tten("dd sn m16", "tm", T.tm[:, :], T.dd[:, :].indirect(T.sn[:, :]), T.m16[:, :], OP.mult)
        scan("tm r16", "ts", T.ts[:, :], T.r16[:, :], T.tm[:, :])
        tten("ts tf", "tg", T.tg[:, :], T.ts[:, 15:704:16], T.tf[:, :], OP.add)
        cp("tg", "tl", T.tl[:, :], T.tg[:, :])
        lo = 0 if r < 2 else 352
        tten("pw tl m16", "tm", T.tm[:, lo:704], T.pw[:, :].indirect(T.tl[:, lo // 16:44]), T.m16[:, lo:704], OP.mult)
        scan("tm r16", "ts", T.ts[:, lo:704], T.r16[:, lo:704], T.tm[:, lo:704])
        if r < 2:
            cp("ts", "sl%d" % (r + 1), T["sl%d" % (r + 1)][:, :], T.ts[:, 15:704:16])
            send_list(r + 1)
            fetch(r + 1)
        ts("ts", "tx", T.tx[:, :], T.ts[:, 367:704:16], 176.0, None, OP.add)
        if r < 2:
            own_lists(r + 1)
        else:
            op("v", "vb", "vq", V.quantize_mx, T.vq[:, :], T.vs[:, :], T.vb[:, :])
        hp = route(topo, partner(r), core)
        for h in range(2):
            a, n = HALF[h]
            arrived("dq%d%d" % (r, h), ("ca%d" if h == 0 else "cb%d") % r, sum(2 * len(topo.engines(k, core)) for k in hp[2 * h:2 * h + 2]))
            for b in range(4):
                k, ps = bank(h, b)
                mm("eq dq%d%d" % (r, h), k, ps, T.eq[:, 128 * b:128 * b + 128], T.es[:, 128 * b:128 * b + 128],
                   T["dq%d" % r][:, a:a + n], T["ds%d" % r][:, a:a + n])
            for b in range(4):
                k, ps = bank(h, b)
                o = T.dw[:, C * b + a:C * b + a + n]
                if h == 0 or b % 2 == 0:
                    act(k, "dw%d%d" % (h, b), o, ps)
                else:
                    cp(k, "dw%d%d" % (h, b), o, ps)
        if r < 2:
            repeat_lists()
        for b in range(4):
            v = slice(64 + b, 1472, 4)
            tten("tx xp%d0 xp%d1 dw0%d dw1%d" % (r, r, b, b), "xp%d0" % (r + 1), T["xp%d" % (r + 1)][:, v], plane(T.dw, b).indirect(T.tx[:, :]), XP[:, v], OP.add)

    act("pw tl", "tw", T.tw[:, :], T.pw[:, :].indirect(T.tl[:, :]), AF.Identity, bias=176.0)
    dma("s", "d_so", "tw", "so", T.so[:, 0:352], T.tw[0:128:16, 352:704])
    dma("s", "d_so", "tw", "so2", T.so[:, 352:704], T.tw[0:128:16, 0:352])
    qx(3, 0)
    qx(3, 1)
    dma("s", "d_oc", "xq0 xq1", "oc", T.oc[:, :], T.xq[:, 16:368].bitcast(dt.uint8))
    for k in range(4):
        dma("s", "d_oc", "xq0 xq1", "osc%d" % k, T.osc[4 * k:4 * k + 4, :], T.xs[32 * k:32 * k + 4, 16:368])
    mm("vq xq0 xq1", "pa0", T.pa[:, 0:C], T.vq[:, :], T.vs[:, :], T.xq[:, 16:368], T.xs[:, 16:368])
    cp("pa0", "yb", T.yb[:, :], T.pa[:, 0:C])
    dma("a", "d_y", "yb", "y", T.y[:, :], T.yb[:, :])
    total["ls"] = sent[0]
    for s in total:
        g.wait_ge(T.sem[s], total[s])
